import numpy as np, ml_dtypes
CORES = [3,7,11,15,131,135,139,143]
N = 8
BF = ml_dtypes.bfloat16
def gentries(a):
    return np.ascontiguousarray(a.reshape(8, 16, -1).transpose(0, 2, 1)).reshape(8, -1)
def gtable(e):
    e = np.asarray(e); return np.ascontiguousarray(e.reshape(8, -1, 16).transpose(0, 2, 1)).reshape(128, -1).astype(np.int32)
R, L, W, RO = 512, 8, 4096, 3
H, SP = L // 2, W // R
def parts(rng):
    X = (rng.integers(0, 256, (N, 8, 16, W)) * rng.integers(64, 257, (N, 8, 1, W))) >> 8
    A = rng.integers(0, W, (N, 8, R, L))
    z = np.maximum(rng.integers(0, 256, (N, 8, 16, R)), rng.integers(0, 256, (N, 8, 1, R)) * rng.integers(0, 2, (N, 8, 1, R)))
    w = rng.integers(0, 256, (N, 8, 16)); T = np.exp2(4 + 5.5 * rng.random((N, 8))).astype(np.int64)
    return X, A, z, w, T
def pack(X, A, z, w, T):
    return {"xd": np.ascontiguousarray(X.reshape(N, 128, W)).astype(np.float32).astype(BF), "ra": np.stack([gtable(a.reshape(8, -1)) for a in A]),
            "zu": np.ascontiguousarray(z.reshape(N, 128, R)).astype(np.float32).astype(BF), "wg": np.ascontiguousarray(w.reshape(N, 128, 1)).astype(np.int32),
            "th": np.repeat(T.reshape(N, 8, 1), 16, axis=2).reshape(N, 128, 1).astype(np.int32)}
def setup_inputs(rng):
    return pack(*parts(rng))
def setup_inputs_ties(rng):
    X, A, z, w, T = parts(rng); m = rng.integers(2, 254 // L + 1, (N, 8)); k = np.arange(L)
    at = rng.integers(0, 16, (N, 8, 1, W)); e = rng.integers(-1, 2, (N, 8, 1, W))
    X = m[:, :, None, None] * (1 + np.arange(W) % L) + e * (np.arange(16)[:, None] == at)
    lev = (2 * k[None, :] + ((np.arange(N) // 2) % 2)[:, None]) % L
    A = L * rng.integers(0, W // L, (N, 8, R, L)) + lev[:, None, None, :]
    o = rng.permutation(8); T = m * np.array([16, 16, 32, 32, 0, 0, 16, 16])[o] + np.array([0, 0, 0, 0, 1, 2, 1, -1])[o]
    z = np.where(rng.random((N, 8, 1, R)) < 0.75, 255, z)
    return pack(X, A, z, w, T)
def setup_inputs_near(rng):
    X0, A, z, w, T = parts(rng); o = [int(v) for v in rng.permutation(8)]; q = [int(v) for v in rng.permutation(N)]; p = (q[1] - 1) % N
    T = rng.integers(2049, 4081, (N, 8)); T[:, o[1]] = 4080; T[:, o[2]] = 2049; T[:, o[3]] = 4 * rng.integers(513, 1020, N)
    e = np.array([-1, 0, 1, -1])[np.arange(W) % 4]
    m = np.maximum(4080 - T[:, :, None] - e, 0)[:, :, None, :]; b = m >> 4
    v = rng.integers(-b, b + 1, (N, 8, 8, W))
    X = 255 - np.concatenate([b + v, b - v], axis=2) - (((np.arange(16)[:, None] + rng.integers(0, 16, (N, 8, 1, W))) & 15) < (m & 15)).astype(np.int64)
    z = np.where(rng.random((N, 8, 1, R)) < 0.75, 255, z); z[p] = 255; z[:, o[0]] = 255
    for r in range(N):
        n = 3 * R - 1 if r == p else int(rng.integers(R, 6 * R))
        yes = (rng.permutation(7 * R) < n).reshape(7, R); c = 4 * rng.integers(0, W // 4, (7, R)); i = rng.integers(0, 2, (7, R))
        A[r, o[1:], :, 0] = np.where(yes, c + 1 + i, np.where(rng.random((7, R)) < 0.5, c + 3 * i, (W - 1) * i))
    X[:, o[0]] = np.arange(W) * 256 // W; T[:, o[0]] = rng.integers(1, 17, N); S = W // (H + 1)
    low = ((np.arange(N) // 2) % 2 == 0)[:, None, None]
    A[:, o[0], :, :H] = np.where(low, 0, S * (1 + np.arange(H)) + rng.integers(0, S // 2, (N, R, H)))
    X[q[0]] = X0[q[0]]; X[q[0], :, :, 31::32] = 255; T[q[0]] = 4080
    for g in range(8):
        f = int(rng.integers(0, 16)); X[q[0], g, f] = np.minimum(X[q[0], g, f], 254)
    return pack(X, A, z, w, T)
def setup_inputs_corners(rng):
    X, A, z, w, T = parts(rng); o = [int(v) for v in rng.permutation(8)]; q = rng.permutation(N)
    A[:, o[0]] = A[:, o[0], :, :1].copy(); T[:, o[0]] = 1
    A[:, o[1]] = rng.choice(np.array([0, W - 1]), (N, R, L))
    z[:, o[2], :, ::2] = 0; z[:, o[2], :, 1::4] = 255; T[:, o[2]] = np.arange(N) % 2
    X[:, o[3], :, ::3] = 255; z[:, o[3]] = 255; T[:, o[3]] = 4080
    w[:, o[4]] = 0
    w[:, o[5]] = 255; z[:, o[5]] = 255; X[:, o[5]] = np.where(rng.random((N, 1, W)) < 0.5, 255, X[:, o[5]])
    A[:, o[6]] = A[0, o[6], 0].copy()
    A[:, o[7]] = np.sort(A[:, o[7]], axis=-1); X[:, o[7]] = np.arange(W) * 240 // W + rng.integers(0, 16, (N, 16, W)); z[:, o[7]] = 255; T[:, o[7]] = 1
    T[q[0]] = 0; T[q[1]] = 4080
    return pack(X, A, z, w, T)
def setup_inputs_ends(rng):
    c = rng.integers(0, 3, (N, 8, 1, W)); X = 255 * np.where(c == 2, rng.integers(0, 2, (N, 8, 16, W)), c)
    X[:, 7, :, W - 1] = 255; X[:, 7, :, 0] = 0; X[:, 3, :, W - 1] = 0; X[:, 3, :, 0] = 255
    p = rng.random((N, 8, R, L)); A = np.where(p < 0.4, 0, np.where(p < 0.8, W - 1, rng.integers(0, W, (N, 8, R, L))))
    c = rng.integers(0, 4, (N, 8, 1, R)); z = 255 * np.where(c == 3, rng.integers(0, 2, (N, 8, 16, R)), (c > 0).astype(np.int64))
    c = rng.integers(0, 3, (N, 8, 1)); w = 255 * np.where(c == 2, rng.integers(0, 2, (N, 8, 16)), c)
    w[:, 7] = 255; w[:, 0, 0] = 0; w[:, 0, 15] = 255
    T = 4080 * rng.integers(0, 2, (N, 8)); T[:, 7] = 4080; T[:, 0] = 0; T[0, 1:7] = 0
    z[:, 7, :, R - 2:] = 255; z[:, 0, :, 0] = 0
    A[:, 7, R - 2, 0] = W - 1; A[:, 7, R - 1] = 0
    A[(np.arange(N) // 2) % 2 == 1, 7, R - 1, H - 1] = W - 1
    return pack(X, A, z, w, T)
def setup_inputs_spread(rng):
    X, A, z, w, T = parts(rng)
    X = (np.exp2(8 * rng.random((N, 8, 1, W))) * rng.random((N, 8, 16, W)) * (rng.random((N, 8, 1, W)) > 0.0625)).astype(np.int64)
    A = np.minimum((W * rng.random((N, 8, R, L)) ** rng.choice(np.array([1.0, 2.0, 6.0]), (N, 8, R, 1))).astype(np.int64), W - 1)
    z = np.where(rng.random((N, 8, 1, R)) < 0.5, z, (np.exp2(8 * rng.random((N, 8, 1, R))) * rng.random((N, 8, 16, R))).astype(np.int64))
    w = np.minimum(np.exp2(8 * rng.random((N, 8, 16))).astype(np.int64) - rng.integers(0, 2, (N, 8, 16)), 255)
    T = np.minimum(np.exp2(12 * rng.random((N, 8))).astype(np.int64) - 1, 4080)
    return pack(X, A, z, w, T)
def check_inputs(d):
    bad = []
    for k, lo, hi in (("xd", 0, 255), ("ra", 0, W - 1), ("zu", 0, 255), ("wg", 0, 255), ("th", 0, 4080)):
        v = np.asarray(d[k]).astype(np.float64)
        if not (np.min(v) >= lo and np.max(v) <= hi): bad.append("range of " + k)
        elif np.any(v != np.floor(v)): bad.append("whole numbers of " + k)
    v = np.asarray(d["th"]).reshape(-1, 16)
    if np.any(v != v[:, :1]): bad.append("th alike in a group")
    return bad
def reference(xd, ra, zu, wg, th):
    X = xd.astype(np.float32).astype(np.int64).reshape(N, 8, 16, W); z = zu.astype(np.float32).astype(np.int64).reshape(N, 8, 16, R)
    A = np.stack([gentries(a) for a in ra]).astype(np.int64).reshape(N, 8, R, L)
    w = wg.astype(np.int64).reshape(N, 8, 16, 1); T = th.astype(np.int64).reshape(N, 8, 16)[:, :, 0]
    turn = [0] * N
    for rnd in range(RO):
        d = 1 + rnd % (N - 2)
        lost = np.zeros((N, 8, R), bool); beaten = np.zeros((N, 8, R), bool); h = np.zeros((N, 8, R), np.int64)
        D1 = np.zeros((N, 8, R, L), np.int64); D2 = np.zeros((N, 8, R, L), np.int64); nz = np.zeros_like(z); nturn = [0] * N
        for q in range(N):
            r = (q - d) % N; s = (q + 1) % N
            C = np.empty((8, R, L), np.int64)
            C[:, :, 0::2] = A[r][:, :, :H]; C[:, :, 1::2] = np.roll(A[s], -turn[q], axis=1)[:, :, :H]
            x = np.take_along_axis(X[q], C.reshape(8, 1, R * L), 2).reshape(8, 16, R, L)
            top = np.maximum.accumulate(np.minimum(x, z[r][:, :, :, None]), axis=3)
            gain = top.copy(); gain[:, :, :, 1:] -= top[:, :, :, :-1]
            click = np.add.reduce(gain, axis=1) >= T[q][:, None, None]
            D = np.take_along_axis(C, np.argsort(~click, axis=2, kind="stable"), 2)
            n = click.astype(np.int64); a = np.add.reduce(n[:, :, 0::2], axis=2); b = np.add.reduce(n[:, :, 1::2], axis=2)
            E = top[:, :, :, L - 1]
            u = np.add.reduce(w[q] * E, axis=1) & 4095
            lost[r] = b > a; D1[r] = D; h[r] = (((u * u) >> 4) + u) & (W - 1)
            beaten[s] = np.roll(a > b, turn[q], axis=1); D2[s] = np.roll(D, turn[q], axis=1)
            nz[r] = np.abs(255 - z[r] - E)
            place = np.arange(R) * SP + (u & (SP - 1))
            np.put_along_axis(X[q], np.repeat(place[:, None, :], 16, axis=1), E, 2)
            nturn[q] = int(np.add.reduce(n.reshape(-1))) % R
        A3 = A.copy(); A3[:, :, :, H - 1] = h
        A = np.where(lost[:, :, :, None], D1, np.where(beaten[:, :, :, None], D2, A3)); z = nz; turn = nturn
    return {"ya": np.stack([gtable(a.reshape(8, -1)) for a in A]).astype(np.float32), "yz": z.reshape(N, 128, R).astype(np.float32)}

@@ -1,0 +1,495 @@
+from concourse.bass import DstId, RemoteDMATransfer
+from concourse.mybir import AluOpType as ALU, ActivationFunctionType as ACT
+
+N, RO = 8, 3
+KK = float(2 ** 21)
+BIG = float(2 ** 24)
+CH = [(0, 16), (16, 32)]
+VROWS = [(0, 2), (0, 2)]
+SORD = (1, 3, 5, 7, 0, 2, 4, 6)
+ZENG = [["SVSVSVSV", "GVGVGVGV"], ["SSGSGSSS", "GGGGGGGG"], ["SSGSGSSS", "GGGGGGGG"]]
+NC = len(CH)
+UPW, UP1, PSPLIT = 0, 2, 1
+LS = 264
+
+F, BF, I32, U16, F16 = "float32", "bfloat16", "int32", "uint16", "float16"
+SCRATCH = {}
+for _dt, _lst in (
+        (BF, dict(X=4096, B0=4736, B1=4736, TOP=4736, zin=512, mst=144, wmst=144, idb=128, idn=128, kb=256, c32=128,
+                  cr0=128, cr1=128, cr2=128, cm32=128, c512=256, dmask=256, click=256, junk=256, diff=288, ua=256, lz0=512, lz1=512, lz2=512, lz3=512,
+                  zn0=512, zn1=512, zn2=512)),
+        (F, dict(raf=256, A8=256, wtf=8, zout=512, a1=128, a2=128, ix=256, pcf=4, e1=384, ones=128, i8=32, jt=30, jk=30, ccs=30,
+                 kp=30, kp0=30, sgn=30, gu0=144, gu1=144, u010=256, u011=256, rp=32, rq=144, LV=8 * LS, uf=32, sq=32, hf=32, cnt=4, tf=4, y0=30,
+                 U=128, ff=256, Y=256, lP0=128, lQ0=128, lP1=128, lQ1=128, P0=256, P1=256, P2=256, Q0=256, Q1=256, Q2=256, zero=128,
+                 lp1_0=128, lp2_0=128, lq_0=128, lu_0=128, lp1_1=128, lp2_1=128, lq_1=128, lu_1=128)),
+        (I32, dict(ra32=256, wt32=8, pc32=4, jk32=30, m1=128, m2=128, a1c=128, a2c=128, v32=32, u32=32, u7=32, pl32=32, t32=4,
+                   y1=30, y2=30, y3=30, f32=256, f33=256)),
+        (U16, dict(off1=128, off2=128, pl=32, ro0=30, ro1=30, ro2=30)),
+        (BF, dict(p01=256)), (F16, dict(a1h=128, a2h=128, gr=144))):
+    for _n, _c in _lst.items():
+        SCRATCH[_n] = ("sbuf", [128, _c], _dt)
+SCRATCH["tr"] = ("sbuf", [128, 2, 8, 2, 8], F)
+SCRATCH["prev"] = ("sbuf", [128, 32, 8], F)
+for _n, _s in (("psS0", [32, 16]), ("psS1", [32, 16]), ("psZ", [512]), ("psV", [512]), ("psK0", [512]), ("psK1", [512]),
+               ("psR", [8, 64]), ("psC", [512])):
+    SCRATCH[_n] = ("psum", [128] + _s, F)
+
+ARR = ["a1", "a2", "lz0", "lz1", "lz2", "lz3", "lP0", "lQ0", "lP1", "lQ1"] + ["%s%d" % (n, t) for t in range(RO - 1) for n in ("lp1_", "lp2_", "lq_", "lu_")]
+SEMAPHORES = ["cV", "cS", "cT", "cG", "sent", "dra", "dzu", "dw", "dt", "dx0", "dx1", "dya", "dyz"] + ["r_" + a for a in ARR]
+
+
+def rank_program(g, core, T, topo):
+    q = T.rank_of(core)
+    if q is None:
+        return
+    cores = T.cores
+    V, S, PE = g.vector, g.scalar, g.tensor
+    eng = {"V": V, "S": S, "T": PE, "G": g, "Y": g.sync}
+    mask = -1
+    for a in cores:
+        for b in cores:
+            if a != b:
+                mask &= topo.mask(a, b)
+    bits = [b for b in range(mask.bit_length()) if mask >> b & 1]
+    neng = len(bits)
+
+    writer, readers, bank, total = {}, {}, {}, {}
+    seen = {e: {} for e in eng}
+    for a in ARR:
+        n = neng // 2 if not PSPLIT and (a in ("a1", "a2") or a.startswith("lp")) else neng
+        writer[a] = ("r_" + a, n)
+        total["r_" + a] = n
+
+    def waits(e, r, w, x):
+        need = {}
+        evs = [writer[t] for t in r]
+        for t in w:
+            evs += [ev for ev in [writer.get(t)] + readers.get(t, []) if ev is not None and not (e == "T" and ev[0] == "cT")]
+        evs += [bank[t] for t in x if t in bank and bank[t][0] != "c" + e]
+        for s, n in evs:
+            need[s] = max(need.get(s, 0), n)
+        for s, n in need.items():
+            if seen[e].get(s, 0) < n:
+                eng[e].wait_ge(T.sem[s], n)
+                seen[e][s] = n
+
+    def note(ev, r, w, x):
+        for t in r:
+            readers.setdefault(t, []).append(ev)
+        for t in w:
+            writer[t] = ev
+            readers[t] = []
+        for t in x:
+            bank[t] = ev
+
+    def op(e, fn, r=(), w=(), x=()):
+        waits(e, r, w, x)
+        s = "c" + e
+        total[s] = total.get(s, 0) + 1
+        fn().then_inc(T.sem[s], 1)
+        note((s, total[s]), r, w, x)
+
+    def dma(e, out, in_, s, r=(), w=()):
+        waits(e, r, w, ())
+        eng[e].dma_start(out, in_).then_inc(T.sem[s], 16)
+        total[s] = 16
+        note((s, 16), r, w, ())
+
+    def send(src, r, dsts):
+        waits("G", r, (), ())
+        trs = []
+        n = len(dsts)
+        for j, (d, name) in enumerate(dsts):
+            rid, pid = topo.addr(cores[d % N], core)
+            m = 0
+            for b in bits[j * neng // n:(j + 1) * neng // n]:
+                m |= 1 << b
+            trs.append(RemoteDMATransfer(dst_ids=[DstId(rid=rid, pnc=pid)], dma_engine_mask=m, remote_sem=T.sem["r_" + name],
+                                         src=src, dsts=[T[name][:]]))
+        g.remote_dma_fused(trs, local_sem=T.sem.sent)
+        total["sent"] = total.get("sent", 0) + neng
+
+    def send2(src, r, dsts):
+        if PSPLIT:
+            for x in dsts:
+                send(src, r, [x])
+        else:
+            send(src, r, dsts)
+
+    def ts(out, in0, s1, o0, s2=None, o1=None):
+        if o1 is None:
+            return lambda: V.tensor_scalar(out, in0, s1, None, o0)
+        return lambda: V.tensor_scalar(out, in0, s1, s2, o0, o1)
+
+    def tt(out, a, b, o):
+        return lambda: V.tensor_tensor(out, a, b, o)
+
+    def cp(out, a):
+        return lambda: V.tensor_copy(out, a)
+
+    def ms(out, v):
+        return lambda: V.memset(out, v)
+
+    def act(out, a, f, **kw):
+        return lambda: S.activation(out, a, f, **kw)
+
+    def scn(out, a, b, init, o0, o1):
+        return lambda: V.tensor_tensor_scan(out, a, b, init, o0, o1)
+
+    def mms(lst):
+        def f():
+            ins = None
+            for o, l, rr, a, b in lst:
+                ins = PE.matmul(o, l, rr, a, b)
+            return ins
+        return f
+
+    def iota(out, pat, base, cm):
+        return lambda: g.iota(out, pat, base, cm, allow_small_or_imprecise_dtypes=True)
+
+    def row(buf, c0, c1, s):
+        a = 144 * c0 + 16 * s
+        return buf[:, a:a + 9 * (16 * (c1 - c0) - 1) + 1:9]
+
+    def lane(buf, c0, c1, m):
+        a = 144 * c0 + 9 * m
+        return buf[:, a:a + 16 * (9 * (c1 - c0) - 1) + 1:16]
+
+    dma("Y", T.ra32[:], T.ra[:], "dra", w=["ra32"])
+    dma("S", T.zin[:], T.zu[:], "dzu", w=["zin"])
+    dma("Y", T.X[:, 0:2048], T.xd[:, 0:2048], "dx0", w=["X0"])
+    dma("S", T.X[:, 2048:4096], T.xd[:, 2048:4096], "dx1", w=["X1"])
+    dma("Y", T.wt32[:, 0:1], T.wg[:], "dw", w=["wg"])
+    dma("Y", T.wt32[:, 4:5], T.th[:], "dt", w=["th"])
+
+    op("G", iota(T.ix[:], [[1, 256]], 0, 0), w=["ix"])
+    op("G", lambda: g.iota(T.pc32[:, 0:1], [[0, 1]], 0, 1), w=["p32"])
+    op("G", iota(T.kb[0:64, :], [[-32, 32], [0, 8]], 0, 0), w=["kb0"])
+    op("G", iota(T.kb[64:128, :], [[0, 32], [2, 8]], -15, 0), r=["ix", "p32", "kb0"], w=["kb1"])
+    op("V", ms(row(T.B0, 0, 32, 0), 0.0), w=["s0a"])
+    op("V", ms(row(T.B1, 0, 32, 0), 0.0), w=["s0b"])
+    for c, (c0, c1) in enumerate(CH):
+        for k in VROWS[c]:
+            op("V", ms(row(T.B1, c0, c1, k + 1), 255.0), w=["k%d_%d" % (c, k)])
+    op("V", ms(T.dmask[:], -1.0), w=["dmask"])
+    op("V", ts(T.pc32[:, 1:2], T.pc32[:, 0:1], 15, ALU.bitwise_and), r=["p32"], w=["m32"])
+    op("V", ms(T.dmask[:, 0:256:8], 0.0), w=["dmask"])
+    op("V", cp(T.pcf[:, 0:2], T.pc32[:, 0:2]), r=["p32", "m32"], w=["pm"])
+    pcol, mcol, gcol, m8 = T.pcf[:, 0:1], T.pcf[:, 1:2], T.pcf[:, 2:3], T.pcf[:, 3:4]
+    op("V", tt(gcol, pcol, mcol, ALU.subtract), r=["pm"], w=["gcol"])
+    op("V", ts(m8, mcol, 8.0, ALU.mult), r=["pm"], w=["m8"])
+
+    send(T.zin[:], ["zin"], [(q + 1, "lz0")])
+    op("V", cp(T.raf[:], T.ra32[:]), r=["ra32"], w=["raf"])
+    for e in range(8):
+        op("V", lambda e=e: V.transpose(T.tr[:, :, e], T.raf[:, e:256:8]), r=["raf"], w=["tr%d" % e])
+    trs8 = ["tr%d" % e for e in range(8)]
+    for k in range(8):
+        op("V", lambda k=k: V.transpose(T.A8[:, 32 * k:32 * k + 32], T.tr[:, :, :, :, k]), r=trs8, w=["A8_%d" % k])
+        if k == 3:
+            send2(T.A8[:, 0:128], ["A8_%d" % j for j in range(4)], [(q - 1, "a2"), (q + 1, "a1")])
+    op("G", iota(T.jt[:], [[0, 3], [16, 10]], 0, 0), r=["kb1"], w=["jt"])
+    for n, a, b, v, tag in (("sgn", 0, 10, 1, "sg0"), ("sgn", 10, 30, -1, "sg1"), ("ccs", 0, 10, 0, "cc0"), ("ccs", 10, 30, 4127, "cc1"),
+                            ("kp0", 0, 10, 256, "kq0"), ("kp0", 10, 20, LS, "kq1"), ("kp0", 20, 30, 0, "kq2")):
+        op("G", iota(T[n][:, a:b], [[0, b - a]], v, 0), w=[tag])
+    op("V", ts(T.mst[:], T.ix[:, 0:144], gcol, ALU.subtract, 15.0, ALU.is_equal), r=["ix", "gcol"], w=["mst"])
+    op("V", cp(T.wtf[:, 0:1], T.wt32[:, 0:1]), r=["wg"], w=["wf"])
+    op("V", cp(T.wtf[:, 4:5], T.wt32[:, 4:5]), r=["th"], w=["tf0"])
+    wcol, tcol = T.wtf[:, 0:1], T.wtf[:, 4:5]
+    op("V", ts(T.idb[:], T.ix[:, 0:128], pcol, ALU.is_equal), r=["ix", "pm"], w=["idb"])
+    op("S", act(T.wmst[:], T.mst[:], ACT.Copy, scale=wcol), r=["mst", "wf"], w=["wmst"])
+    op("S", act(T.idn[:], T.idb[:], ACT.Copy, scale=-32768.0), r=["idb"], w=["idn"])
+    for h in range(2):
+        op("S", act(T.i8[:, 16 * h:16 * h + 16], T.ix[:, 0:16], ACT.Identity, scale=128.0, bias=m8), r=["ix", "m8"], w=["i8"])
+    op("S", act(T.u010[:, 0:128], T.idb[:], ACT.Copy), r=["idb"], w=["u010"])
+    g4 = T.wtf[:, 1:2]
+    op("S", act(g4, gcol, ACT.Copy, scale=4.0), r=["gcol"], w=["g4"])
+    for n, v in (("c32", 32.0), ("cr0", 96.0), ("c512", 512.0), ("cm32", -32.0), ("diff", 0.0), ("zero", 0.0), ("ones", 1.0)):
+        op("V", ms(T[n][:], v), w=[n])
+
+    late = [
+        lambda: op("V", ts(T.jt[:], T.jt[:], mcol, ALU.add), r=["jt", "pm"], w=["jt"]),
+        lambda: op("V", ms(T.cr1[:], 160.0), w=["cr1"]),
+        lambda: op("V", ts(T.jk[:], T.jt[:], 1.0 / 33, ALU.mult, -0.485, ALU.add), r=["jt"], w=["jk"]),
+        lambda: op("V", tt(T.ccs[:], T.ccs[:], T.jt[:], ALU.add), r=["cc0", "cc1", "jt"], w=["ccs"]),
+        lambda: op("V", cp(T.jk32[:], T.jk[:]), r=["jk"], w=["jk32"]),
+        lambda: op("V", ms(T.cr2[:], 224.0), w=["cr2"]),
+        lambda: op("V", ts(T.jk[:], T.jk32[:], 3.0, ALU.min), r=["jk32"], w=["jk"]),
+        lambda: op("V", ts(T.jt[:], T.jk32[:], -33.0, ALU.mult), r=["jk32"], w=["jt"]),
+        lambda: op("V", tt(T.kp[:], T.jk[:], T.kp0[:], ALU.mult), r=["jk", "kq0", "kq1", "kq2"], w=["kp"]),
+        lambda: op("V", tt(T.ccs[:], T.ccs[:], T.jt[:], ALU.add), r=["ccs", "jt"], w=["ccs"]),
+        lambda: op("V", ts(T.ccs[:], T.ccs[:], 8.0, ALU.mult), r=["ccs"], w=["ccs"]),
+        lambda: op("V", cp(T.y1[:], T.ccs[:]), r=["ccs"], w=["y1"])]
+
+    psS = [T.psS0, T.psS1]
+    srows = [[k for k in SORD if k not in VROWS[c]] for c in range(NC)]
+
+    def zcopy(t, c):
+        c0, c1 = CH[c]
+        lz = "lz%d" % t
+        for k, e in zip(srows[c], ZENG[t][c]):
+            o, i = row(T.B1, c0, c1, k + 1), T[lz][:, 16 * c0:16 * c1]
+            if e == "S":
+                fn = act(o, i, ACT.Copy)
+            elif e == "V":
+                fn = cp(o, i)
+            else:
+                fn = lambda o=o, i=i: g.affine_select(o, i, [[0, 16 * (c1 - c0)]], ALU.is_ge, 0.0, 0, 0)
+            op(e, fn, r=[lz], w=["z%d_%d" % (c, k)])
+
+    def off(k, c):
+        c0, c1 = CH[c]
+        o = T.off2 if k & 1 else T.off1
+        return T.X[:, 0:4096].indirect(o[:, 32 * (k >> 1) + c0:32 * (k >> 1) + c1]), ("off2" if k & 1 else "off1")
+
+    def sgather(c):
+        c0, c1 = CH[c]
+        for k in srows[c]:
+            w, tag = off(k, c)
+            op("S", act(row(T.B0, c0, c1, k + 1), w, ACT.Copy), r=[tag, "X0", "X1"], w=["x%d_%d" % (c, k)])
+
+    def vgather(t, c):
+        c0, c1 = CH[c]
+        lz = "lz%d" % t
+        for k in VROWS[c]:
+            w, tag = off(k, c)
+            op("V", tt(row(T.B0, c0, c1, k + 1), w, T[lz][:, 16 * c0:16 * c1], ALU.min), r=[tag, "X0", "X1", lz], w=["x%d_%d" % (c, k)])
+
+    def scan(t, c):
+        c0, c1 = CH[c]
+        for m in range(16):
+            op("V", scn(lane(T.TOP, c0, c1, m), lane(T.B0, c0, c1, m), lane(T.B1, c0, c1, m), 0.0, ALU.max, ALU.min),
+               r=["x%d_%d" % (c, k) for k in range(8)] + ["z%d_%d" % (c, k) for k in srows[c]] + ["k%d_%d" % (c, k) for k in VROWS[c]] + ["s0a", "s0b"],
+               w=["top%d_%d" % (c, m)])
+            op("T", mms([(psS[c][:, 0:c1 - c0, 0:9], T.mst[:, 15 - m:143 - m], lane(T.TOP, c0, c1, m), m == 0, m == 15)]),
+               r=["top%d_%d" % (c, m), "mst"], w=["S%d" % c], x=["bS%d" % c])
+
+    tops = ["top%d_%d" % (c, m) for c in range(NC) for m in range(16)]
+    clicks = ["click%d" % c for c in range(NC)]
+
+    def vmm(h):
+        op("T", mms([(T.psV[:, 0:32], T.wmst[:, 15 - m:143 - m], T.TOP[:, 128 + 9 * m:4736:144], m == 0, m == 15)
+                     for m in (range(6), range(6, 16))[h]]), r=tops + ["wmst"], w=["v"], x=["bV"])
+
+    def zabs(t, c):
+        a, b = 16 * CH[c][0], 16 * CH[c][1]
+        op("S", act(T["zn%d" % t][:, a:b], T.psZ[:, a:b], ACT.Abs, bias=255.0, scale=-1.0), r=["Z%d" % c], w=["zn%d_%d" % (t, c)], x=["bZ"])
+
+    def zmm(t, c):
+        c0, c1 = CH[c]
+        lz = "lz%d" % t
+        o = T.psZ[:, 16 * c0:16 * c1]
+        op("T", mms([(o, T.idb[:], T[lz][:, 16 * c0:16 * c1], True, False), (o, T.idb[:], row(T.TOP, c0, c1, 8), False, True)]),
+           r=["top%d_%d" % (c, m) for m in range(16)] + ["idb", lz], w=["Z%d" % c], x=["bZ"])
+
+    def prevt(c):
+        c0, c1 = CH[c]
+        op("S", act(T.prev[:, c0:c1, :], psS[c][:, 0:c1 - c0, 0:8], ACT.Identity, bias=tcol),
+           r=["S%d" % c, "tf0"], w=["prev%d" % c], x=["bS%d" % c])
+
+    def click(c):
+        c0, c1 = CH[c]
+        op("V", tt(T.click[:, 8 * c0:8 * c1], psS[c][:, 0:c1 - c0, 1:9], T.prev[:, c0:c1, :], ALU.is_ge),
+           r=["S%d" % c, "prev%d" % c], w=["click%d" % c], x=["bS%d" % c])
+
+    def level(t, j):
+        k = "K%d" % (t & 1)
+        a = LS * j + 8
+        prev = T.ix[:] if j == 0 else T.LV[:, a - LS - 1:a - LS + 255]
+        op("V", scn(T.LV[:, a:a + 256], T["ps" + k][:, 0:256], prev, BIG, ALU.min, ALU.max),
+           r=[k, "ix" if j == 0 else "L%d" % (j - 1), "lv0" if j < 4 else "lv1"], w=["L%d" % j], x=["b" + k])
+
+    def pp(t, j):
+        a = LS * j + 15
+        op("V", tt(T["P%d" % t][:, 32 * j:32 * j + 32], T.LV[:, a:a + 249:8], T.rp[:], ALU.subtract), r=["L%d" % j, "rp"], w=["P%d_%d" % (t, j)])
+
+    def unroll(t, h):
+        gu, u01, ro = T["gu%d" % h], T["u01%d" % (t & 1)], T["ro%d" % t]
+        o = T.psR[:, 4 * h:4 * h + 4, 0:33]
+        op("T", mms([(o, T.cm32[:], T.c512[:, 0:132], True, False)]), r=["cm32", "c512"], w=["R%d" % h], x=["bR"])
+        op("V", tt(gu[:], T.LV[:, 4 * LS * h:4 * LS * (h + 1)].indirect(ro[:, 10:19]), T.rq[:], ALU.subtract),
+           r=["L%d" % (4 * h + j) for j in range(4)] + ["ro%d" % t, "rq"], w=["gu%d" % h])
+        op("T", mms([(o, u01[:, 0:128], gu[:, 1:133], False, t == 0), (o, u01[:, 128:256], gu[:, 0:132], False, True)][:2 if t else 1]),
+           r=["gu%d" % h, "u01%d" % (t & 1)], w=["R%d" % h], x=["bR"])
+
+    def upper(t):
+        Q = T["Q%d" % t]
+        old, tag = (T.zero[:], "zero") if t == 0 else (T["Q%d" % (t - 1)][:, 128:256], "Q%d_hi" % (t - 1))
+        st = [lambda: level(t, 4), lambda: level(t, 5), lambda: pp(t, 4), lambda: level(t, 6), lambda: pp(t, 5), lambda: level(t, 7),
+              lambda: pp(t, 6), lambda: pp(t, 7)]
+        st.append(lambda: send(T["P%d" % t][:, 128:256], ["P%d_%d" % (t, j) for j in range(4, 8)], [(q - t - 1, "lu_%d" % t if t < RO - 1 else "lP1")]))
+        st.append(lambda: unroll(t, 1))
+        st.append(lambda: op("V", tt(Q[:, 128:256], T.psR[:, 4:8, 0:32], old, ALU.max), r=["R1", tag], w=["Q%d_hi" % t], x=["bR"]))
+        return st
+
+    def turn(t):
+        ro, u01 = T["ro%d" % t], T["u01%d" % (t & 1)]
+        tot, ttag, x = T.psC[:, 0:1], "tot", ["bC"]
+        st = [lambda: op("V", cp(T.t32[:, 0:1], tot), r=[ttag], w=["t32"], x=x),
+              lambda: op("V", ts(T.t32[:, 1:2], T.t32[:, 0:1], 4, ALU.logical_shift_right), r=["t32"], w=["tc32"]),
+              lambda: op("V", ts(T.tf[:, 0:1], T.t32[:, 1:2], 8.0, ALU.mult), r=["tc32"], w=["tc"]),
+              lambda: op("S", act(T.y0[:], T.sgn[:], ACT.Copy, scale=T.tf[:, 0:1]), r=["sg0", "sg1", "tc"], w=["y0"]),
+              lambda: op("V", ts(T.tf[:, 1:2], T.t32[:, 1:2], -16.0, ALU.mult, tot, ALU.add), r=["tc32", ttag], w=["tm"], x=x),
+              lambda: op("S", act(T.tf[:, 3:4], T.tf[:, 1:2], ACT.Identity, bias=g4, scale=-1.0), r=["g4", "tm"], w=["tmn"]),
+              lambda: op("S", act(T.ua[:], T.e1[:, 0:256], ACT.Abs, bias=T.tf[:, 3:4]), r=["e1", "tmn"], w=["ua"]),
+              lambda: op("S", act(T.p01[:], T.ua[:], ACT.Relu, bias=1.0, scale=-1.0), r=["ua"], w=["p01"]),
+              lambda: op("V", tt(T.y1[:], T.y0[:], T.ccs[:], ALU.add), r=["y0", "ccs"], w=["y1"]),
+              lambda: op("V", ts(T.y2[:], T.y1[:], 248, ALU.bitwise_and), r=["y1"], w=["y2"]),
+              lambda: op("V", tt(T.y3[:], T.y2[:], T.kp[:], ALU.add), r=["y2", "kp"], w=["y3"]),
+              lambda: t > 0 and op("V", ts(ro[:, 0:10], T.y3[:, 0:10], 0.125, ALU.mult), r=["y3"], w=["rr%d" % t]),
+              lambda: op("V", ts(ro[:, 10:30], T.y3[:, 10:30], 15.0, ALU.add), r=["y3"], w=["ro%d" % t]),
+              lambda: op("S", act(T.tf[:, 2:3], T.tf[:, 1:2], ACT.Identity, bias=g4), r=["g4", "tm"], w=["tmg"]),
+              lambda: op("S", act(T.ua[:], T.e1[:, 128:384], ACT.Abs, bias=T.tf[:, 2:3]), r=["e1", "tmg"], w=["ua"]),
+              lambda: op("S", act(u01[:], T.ua[:], ACT.Relu, bias=1.0, scale=-1.0), r=["ua"], w=["u01%d" % (t & 1)])]
+        return st
+
+    up = late + turn(0)[9:13]
+    for c in range(NC):
+        zcopy(0, c)
+    op("G", iota(T.LV[:, 0:4 * LS], [[0, 4 * LS]], 16000000, 0), w=["lv0"])
+    op("G", iota(T.LV[:, 4 * LS:8 * LS], [[0, 4 * LS]], 16000000, 0), w=["lv1"])
+    op("G", iota(T.e1[:], [[-16, 3], [-80, 8], [-1, 16]], 16, 1), w=["e1"])
+
+    for t in range(RO):
+        d = t + 1
+        last = t == RO - 1
+        P, Q, ro = T["P%d" % t], T["Q%d" % t], T["ro%d" % t]
+        kt = "K%d" % (t & 1)
+        psK = T["ps" + kt]
+        kgrp = [(psK[:, 0:256], T.c32[:], T.kb[:], True, False), (psK[:, 0:256], T["cr%d" % t][:], T.c512[:], False, False)]
+        if t == 0:
+            op("V", cp(T.off2[:], T.a2[:]), r=["a2"], w=["off2"])
+            op("V", cp(T.off1[:], T.a1[:]), r=["a1"], w=["off1"])
+            op("V", ts(T.a2h[:], T.a2[:], -2048.0, ALU.add), r=["a2"], w=["a2h"])
+            op("V", ts(T.a1h[:], T.a1[:], -2048.0, ALU.add), r=["a1"], w=["a1h"])
+            op("V", ms(T.a2[:, 96:128], 0.0), w=["a2"])
+            ap, aptag = T.a2, "a2"
+            kgrp += [(psK[:, 2 * k + 1:256:8], T.idb[:], T.a2h[:, 32 * k:32 * k + 32], False, False) for k in range(4)]
+            ktags = ["a2h"]
+        else:
+            p = t - 1
+            op("V", tt(T.m2[:], T["lp2_%d" % p][:], T["Q%d" % p][:, 0:128], ALU.max), r=["lp2_%d" % p, "Q%d_lo" % p], w=["m2"])
+            fin[0]()
+            op("V", ts(T.a2c[:], T.m2[:], 4095, ALU.bitwise_and), r=["m2"], w=["a2c"])
+            fin[1]()
+            op("V", ts(T.gr[:], T.a2c[:, 0:128].indirect(ro[:, 0:9]), -2048.0, ALU.add), r=["a2c", "rr%d" % t], w=["gr"])
+            o = T.psR[:, 0:4, 0:33]
+            op("T", mms([(o, T.p01[:, 128:256], T.gr[:, 0:132], True, False), (o, T.p01[:, 0:128], T.gr[:, 1:133], False, True)]),
+               r=["gr", "p01"], w=["R0"], x=["bR"])
+            if up:
+                up.pop(0)()
+            op("V", ts(T.off2[:], T.psR[:, 0:4, 0:32], 2048.0, ALU.add), r=["R0"], w=["off2"], x=["bR"])
+            op("V", tt(T.m1[:], T["lp1_%d" % p][:], T["lq_%d" % p][:], ALU.max), r=["lp1_%d" % p, "lq_%d" % p], w=["m1"])
+            op("G", lambda: g.iota(T.a2c[:, 96:128], [[0, 32]], 0, 0), w=["a2c"])
+            op("V", ts(T.a1c[:], T.m1[:], 4095, ALU.bitwise_and), r=["m1"], w=["a1c"])
+            op("V", ts(T.a1h[:], T.a1c[:], -2048.0, ALU.add), r=["a1c"], w=["a1h"])
+            op("V", ts(T.off1[:], T.a1h[:], 2048.0, ALU.add), r=["a1h"], w=["off1"])
+            ap, aptag = T.a2c, "a2c"
+            for k in range(4):
+                kgrp += [(psK[:, 2 * k + 1:256:8], T.p01[:, 128:256], T.gr[:, 33 * k:33 * k + 32], False, False),
+                         (psK[:, 2 * k + 1:256:8], T.p01[:, 0:128], T.gr[:, 33 * k + 1:33 * k + 33], False, False)]
+            ktags = ["gr", "p01"]
+        kgrp += [(psK[:, 2 * k:256:8], T.idb[:], T.a1h[:, 32 * k:32 * k + 32], False, False) for k in range(4)]
+        op("T", mms(kgrp), r=ktags + ["a1h", "idb", "c32", "kb0", "kb1", "c512", "cr%d" % t], w=[kt], x=["b" + kt])
+
+        for c in range(NC):
+            sgather(c)
+        for c in range(NC):
+            vgather(t, c)
+        n1 = UP1 if t else 8
+        for s in up[:n1]:
+            s()
+        for c in range(NC):
+            if c == NC - 1:
+                for s in up[n1:]:
+                    s()
+            scan(t, c)
+            if c < NC - 1:
+                zmm(t, c)
+                prevt(c)
+                zabs(t, c)
+        prevt(NC - 1)
+        zmm(t, NC - 1)
+        vmm(0)
+        for c in range(NC):
+            click(c)
+        op("T", mms([(psK[:, 0:256], T.idn[:], T.click[:], False, True)]), r=clicks + ["idn"], w=[kt], x=["b" + kt])
+        vmm(1)
+        zabs(t, NC - 1)
+        send(T["zn%d" % t][:], ["zn%d_%d" % (t, c) for c in range(NC)], [(q - d if last else q + 1, "lz%d" % (t + 1))])
+        op("V", scn(T.diff[:, 8:264], T.dmask[:], T.click[:], 0.0, ALU.mult, ALU.add), r=clicks + ["dmask"], w=["diff"])
+        op("S", act(T.rp[:], T.diff[:, 15:264:8], ACT.Relu, bias=BIG, scale=-BIG), r=["diff"], w=["rp"])
+        op("S", act(T.rq[:], T.diff[:, 0:288].indirect(ro[:, 20:29]), ACT.Relu, bias=BIG, scale=BIG), r=["diff", "ro%d" % t], w=["rq"])
+        if not last:
+            op("S", act(T.junk[:], T.click[:], ACT.Identity, accum_out=T.cnt[:, 0:1]), r=clicks, w=["cnt", "junk"])
+            op("T", mms([(T.psC[:, 0:1], T.ones[:], T.cnt[:, 0:1], True, True)]), r=["ones", "cnt"], w=["tot"], x=["bC"])
+        level(t, 0)
+        op("V", cp(T.v32[:], T.psV[:, 0:32]), r=["v"], w=["v32"], x=["bV"])
+        level(t, 1)
+        op("V", ts(T.u32[:], T.v32[:], 4095, ALU.bitwise_and), r=["v32"], w=["u32"])
+        level(t, 2)
+        op("V", cp(T.uf[:], T.u32[:]), r=["u32"], w=["uf"])
+        op("S", act(T.sq[:], T.uf[:], ACT.Square, bias=2.0, scale=0.25), r=["uf"], w=["sq"])
+        op("S", act(T.hf[:], T.sq[:], ACT.Identity, bias=-4.25), r=["sq"], w=["hf"])
+        level(t, 3)
+        pp(t, 0)
+        pp(t, 3)
+        pp(t, 1)
+        pp(t, 2)
+        op("V", tt(P[:, 96:128], P[:, 96:128], T.hf[:], ALU.max), r=["P%d_3" % t, "hf"], w=["P%d_3" % t])
+        unroll(t, 0)
+        qlo = lambda: op("V", tt(Q[:, 0:128], T.psR[:, 0:4, 0:32], ap[:], ALU.max), r=["R0", aptag], w=["Q%d_lo" % t], x=["bR"])
+        if not last:
+            send2(P[:, 0:128], ["P%d_%d" % (t, j) for j in range(4)], [(q - d - 1, "lp2_%d" % t), (q + 1, "lp1_%d" % t)])
+            st = turn(t + 1)
+            op("V", ts(T.u7[:], T.v32[:], 7, ALU.bitwise_and), r=["v32"], w=["u7"])
+            st[0]()
+            op("V", tt(T.pl32[:], T.u7[:], T.i8[:], ALU.add), r=["u7", "i8"], w=["pl32"])
+            st[1]()
+            op("V", cp(T.pl[:], T.pl32[:]), r=["pl32"], w=["pl"])
+            qlo()
+            send(Q[:, 0:128], ["Q%d_lo" % t], [(q + d + 2, "lq_%d" % t)])
+            for s in st[2:8]:
+                s()
+            for h in range(2):
+                st[8 + h]()
+                op("V", cp(T.X[:, 2048 * h:2048 * h + 2048].indirect(T.pl[:, 16 * h:16 * h + 16]), row(T.TOP, 16 * h, 16 * h + 16, 8)),
+                   r=tops + ["pl"], w=["X%d" % h])
+            st[10]()
+            zcopy(t + 1, 0)
+            for s in st[13:]:
+                s()
+            fin = st[11:13]
+            up = upper(t)
+            for s in up[:UPW]:
+                s()
+            up = up[UPW:]
+            for c in range(1, NC):
+                zcopy(t + 1, c)
+        else:
+            send(P[:, 0:128], ["P%d_%d" % (t, j) for j in range(4)], [(q - d, "lP0")])
+            up = upper(t)
+            up[2:2] = [qlo, lambda: send(Q[:, 0:128], ["Q2_lo"], [(q + 1, "lQ0")])]
+            for s in up:
+                s()
+            send(Q[:, 128:256], ["Q2_hi"], [(q + 1, "lQ1")])
+
+    op("S", act(T.zout[:], T.lz3[:], ACT.Copy), r=["lz3"], w=["zout"])
+    dma("S", T.yz[:], T.zout[:], "dyz", r=["zout"])
+    op("V", tt(T.U[:], T.lu_0[:], T.A8[:, 128:256], ALU.max), r=["lu_0"] + ["A8_%d" % j for j in range(4, 8)], w=["U"])
+    op("V", tt(T.U[:], T.lu_1[:], T.U[:], ALU.max), r=["lu_1", "U"], w=["U"])
+    for h in range(2):
+        b = slice(128 * h, 128 * h + 128)
+        if h == 1:
+            op("V", tt(T.U[:], T.lP1[:], T.U[:], ALU.max), r=["lP1", "U"], w=["U"])
+        op("V", tt(T.f32[:, b], T.U[:] if h else T.lP0[:], T["lQ%d" % h][:], ALU.max), r=["U" if h else "lP0", "lQ%d" % h], w=["f32_%d" % h])
+        op("V", ts(T.f33[:, b], T.f32[:, b], 4095, ALU.bitwise_and), r=["f32_%d" % h], w=["f33_%d" % h])
+        op("V", cp(T.ff[:, b], T.f33[:, b]), r=["f33_%d" % h], w=["ff%d" % h])
+        for k in range(4 * h, 4 * h + 4):
+            op("V", lambda k=k: V.transpose(T.tr[:, :, :, :, k], T.ff[:, 32 * k:32 * k + 32]), r=["ff%d" % h], w=["ts%d" % k] + (trs8 if k == 0 else []))
+    for e in range(8):
+        op("V", lambda e=e: V.transpose(T.Y[:, e:256:8], T.tr[:, :, e]), r=["ts%d" % k for k in range(8)], w=["Y%d" % e])
+    dma("Y", T.ya[:], T.Y[:], "dya", r=["Y%d" % e for e in range(8)])
+    for s, n in total.items():
+        if seen["G"].get(s, 0) < n:
+            g.wait_ge(T.sem[s], n)

@@ -4,27 +4,28 @@ from concourse.mybir import AluOpType as ALU, ActivationFunctionType as ACT
 N, RO = 8, 3
 KK = float(2 ** 21)
 BIG = float(2 ** 24)
-CH = [(0, 16), (16, 32)]
+CH = [(0, 18), (18, 32)]
+VR0 = [(0, 2, 4), (0, 2, 4)]
 VROWS = [(0, 2), (0, 2)]
 SORD = (1, 3, 5, 7, 0, 2, 4, 6)
-ZENG = [["SVSVSVSV", "GVGVGVGV"], ["SSGSGSSS", "GGGGGGGG"], ["SSGSGSSS", "GGGGGGGG"]]
+ZENG = [["SVSVSVSV", "GGGGGGGG"], ["SSGSGSSS", "GGGGGGGG"], ["SSGSGSSS", "GGGGGGGG"]]
 NC = len(CH)
-UPW, UP1, PSPLIT = 0, 2, 1
+UP1, PSPLIT = 3, 1
 LS = 264
 
 F, BF, I32, U16, F16 = "float32", "bfloat16", "int32", "uint16", "float16"
 SCRATCH = {}
 for _dt, _lst in (
         (BF, dict(X=4096, B0=4736, B1=4736, TOP=4736, zin=512, mst=144, wmst=144, idb=128, idn=128, kb=256, c32=128,
-                  cr0=128, cr1=128, cr2=128, cm32=128, c512=256, dmask=256, click=256, junk=256, diff=288, ua=256, lz0=512, lz1=512, lz2=512, lz3=512,
+                  cr0=128, cr1=128, cr2=128, c512=256, dmask=256, click=256, junk=256, diff=288, ua=256, lz0=512, lz1=512, lz2=512, lz3=512,
                   zn0=512, zn1=512, zn2=512)),
-        (F, dict(raf=256, A8=256, wtf=8, zout=512, a1=128, a2=128, ix=256, pcf=4, e1=384, ones=128, i8=32, jt=30, jk=30, ccs=30,
-                 kp=30, kp0=30, sgn=30, gu0=144, gu1=144, u010=256, u011=256, rp=32, rq=144, LV=8 * LS, uf=32, sq=32, hf=32, cnt=4, tf=4, y0=30,
+        (F, dict(raf=256, A8=256, wtf=8, zout=512, a2=128, ix=256, pcf=4, e1=384, ones=128, i8=32, jt=30, jk=30, ccs=30,
+                 kp=30, kp0=30, sgn=30, gu0=144, gu1=144, u010=256, u011=256, rp=32, rq=144, nrq=144, LV=8 * LS, uf=32, sq=32, hf=32, cnt=4, tf=4, y0=30,
                  U=128, ff=256, Y=256, lP0=128, lQ0=128, lP1=128, lQ1=128, P0=256, P1=256, P2=256, Q0=256, Q1=256, Q2=256, zero=128,
                  lp1_0=128, lp2_0=128, lq_0=128, lu_0=128, lp1_1=128, lp2_1=128, lq_1=128, lu_1=128)),
         (I32, dict(ra32=256, wt32=8, pc32=4, jk32=30, m1=128, m2=128, a1c=128, a2c=128, v32=32, u32=32, u7=32, pl32=32, t32=4,
                    y1=30, y2=30, y3=30, f32=256, f33=256)),
-        (U16, dict(off1=128, off2=128, pl=32, ro0=30, ro1=30, ro2=30)),
+        (U16, dict(off1=128, off2=128, a16=128, pl=32, ro0=30, ro1=30, ro2=30)),
         (BF, dict(p01=256)), (F16, dict(a1h=128, a2h=128, gr=144))):
     for _n, _c in _lst.items():
         SCRATCH[_n] = ("sbuf", [128, _c], _dt)
@@ -34,7 +35,7 @@ for _n, _s in (("psS0", [32, 16]), ("psS1", [32, 16]), ("psZ", [512]), ("psV", [
                ("psR", [8, 64]), ("psC", [512])):
     SCRATCH[_n] = ("psum", [128] + _s, F)
 
-ARR = ["a1", "a2", "lz0", "lz1", "lz2", "lz3", "lP0", "lQ0", "lP1", "lQ1"] + ["%s%d" % (n, t) for t in range(RO - 1) for n in ("lp1_", "lp2_", "lq_", "lu_")]
+ARR = ["off1", "off2", "lP0", "lQ0", "lP1", "lQ1"] + ["lz%d_%d" % (t, c) for t in range(RO + 1) for c in range(NC)] + ["%s%d" % (n, t) for t in range(RO - 1) for n in ("lp1_", "lp2_", "lq_", "lu_")]
 SEMAPHORES = ["cV", "cS", "cT", "cG", "sent", "dra", "dzu", "dw", "dt", "dx0", "dx1", "dya", "dyz"] + ["r_" + a for a in ARR]
 
 
@@ -56,7 +57,7 @@ def rank_program(g, core, T, topo):
     writer, readers, bank, total = {}, {}, {}, {}
     seen = {e: {} for e in eng}
     for a in ARR:
-        n = neng // 2 if not PSPLIT and (a in ("a1", "a2") or a.startswith("lp")) else neng
+        n = neng // 2 if not PSPLIT and (a in ("off1", "off2") or a.startswith("lp")) else neng
         writer[a] = ("r_" + a, n)
         total["r_" + a] = n
 
@@ -95,7 +96,7 @@ def rank_program(g, core, T, topo):
         total[s] = 16
         note((s, 16), r, w, ())
 
-    def send(src, r, dsts):
+    def send(src, r, dsts, dst=None):
         waits("G", r, (), ())
         trs = []
         n = len(dsts)
@@ -105,9 +106,13 @@ def rank_program(g, core, T, topo):
             for b in bits[j * neng // n:(j + 1) * neng // n]:
                 m |= 1 << b
             trs.append(RemoteDMATransfer(dst_ids=[DstId(rid=rid, pnc=pid)], dma_engine_mask=m, remote_sem=T.sem["r_" + name],
-                                         src=src, dsts=[T[name][:]]))
+                                         src=src, dsts=[T[name][:] if dst is None else dst]))
         g.remote_dma_fused(trs, local_sem=T.sem.sent)
         total["sent"] = total.get("sent", 0) + neng
+
+    def sendz(src, r, d, t, c):
+        a, b = 16 * CH[c][0], 16 * CH[c][1]
+        send(src[:, a:b], r, [(d, "lz%d_%d" % (t, c))], T["lz%d" % t][:, a:b])
 
     def send2(src, r, dsts):
         if PSPLIT:
@@ -169,8 +174,8 @@ def rank_program(g, core, T, topo):
     op("V", ms(row(T.B0, 0, 32, 0), 0.0), w=["s0a"])
     op("V", ms(row(T.B1, 0, 32, 0), 0.0), w=["s0b"])
     for c, (c0, c1) in enumerate(CH):
-        for k in VROWS[c]:
-            op("V", ms(row(T.B1, c0, c1, k + 1), 255.0), w=["k%d_%d" % (c, k)])
+        for k in VR0[c]:
+            op("V", ms(row(T.B1, c0, c1, k + 1), 255.0), w=["z%d_%d" % (c, k)])
     op("V", ms(T.dmask[:], -1.0), w=["dmask"])
     op("V", ts(T.pc32[:, 1:2], T.pc32[:, 0:1], 15, ALU.bitwise_and), r=["p32"], w=["m32"])
     op("V", ms(T.dmask[:, 0:256:8], 0.0), w=["dmask"])
@@ -179,7 +184,7 @@ def rank_program(g, core, T, topo):
     op("V", tt(gcol, pcol, mcol, ALU.subtract), r=["pm"], w=["gcol"])
     op("V", ts(m8, mcol, 8.0, ALU.mult), r=["pm"], w=["m8"])
 
-    send(T.zin[:], ["zin"], [(q + 1, "lz0")])
+    sendz(T.zin, ["zin"], q + 1, 0, 0)
     op("V", cp(T.raf[:], T.ra32[:]), r=["ra32"], w=["raf"])
     for e in range(8):
         op("V", lambda e=e: V.transpose(T.tr[:, :, e], T.raf[:, e:256:8]), r=["raf"], w=["tr%d" % e])
@@ -187,11 +192,16 @@ def rank_program(g, core, T, topo):
     for k in range(8):
         op("V", lambda k=k: V.transpose(T.A8[:, 32 * k:32 * k + 32], T.tr[:, :, :, :, k]), r=trs8, w=["A8_%d" % k])
         if k == 3:
-            send2(T.A8[:, 0:128], ["A8_%d" % j for j in range(4)], [(q - 1, "a2"), (q + 1, "a1")])
-    op("G", iota(T.jt[:], [[0, 3], [16, 10]], 0, 0), r=["kb1"], w=["jt"])
+            op("V", cp(T.a16[:], T.A8[:, 0:128]), r=["A8_%d" % j for j in range(4)], w=["a16"])
+            send2(T.a16[:], ["a16"], [(q - 1, "off2"), (q + 1, "off1")])
+            sendz(T.zin, ["zin"], q + 1, 0, 1)
+    op("G", iota(T.LV[:, 0:4 * LS], [[0, 4 * LS]], 16000000, 0), r=["kb1"], w=["lv0"])
+    op("G", iota(T.LV[:, 4 * LS:8 * LS], [[0, 4 * LS]], 16000000, 0), w=["lv1"])
+    for j in range(3):
+        op("S", act(T.jt[:, 10 * j:10 * j + 10], T.ix[:, 0:10], ACT.Identity, scale=16.0, bias=mcol), r=["ix", "pm"], w=["jt%d" % j])
     for n, a, b, v, tag in (("sgn", 0, 10, 1, "sg0"), ("sgn", 10, 30, -1, "sg1"), ("ccs", 0, 10, 0, "cc0"), ("ccs", 10, 30, 4127, "cc1"),
                             ("kp0", 0, 10, 256, "kq0"), ("kp0", 10, 20, LS, "kq1"), ("kp0", 20, 30, 0, "kq2")):
-        op("G", iota(T[n][:, a:b], [[0, b - a]], v, 0), w=[tag])
+        op("V", ms(T[n][:, a:b], float(v)), w=[tag])
     op("V", ts(T.mst[:], T.ix[:, 0:144], gcol, ALU.subtract, 15.0, ALU.is_equal), r=["ix", "gcol"], w=["mst"])
     op("V", cp(T.wtf[:, 0:1], T.wt32[:, 0:1]), r=["wg"], w=["wf"])
     op("V", cp(T.wtf[:, 4:5], T.wt32[:, 4:5]), r=["th"], w=["tf0"])
@@ -204,30 +214,30 @@ def rank_program(g, core, T, topo):
     op("S", act(T.u010[:, 0:128], T.idb[:], ACT.Copy), r=["idb"], w=["u010"])
     g4 = T.wtf[:, 1:2]
     op("S", act(g4, gcol, ACT.Copy, scale=4.0), r=["gcol"], w=["g4"])
-    for n, v in (("c32", 32.0), ("cr0", 96.0), ("c512", 512.0), ("cm32", -32.0), ("diff", 0.0), ("zero", 0.0), ("ones", 1.0)):
-        op("V", ms(T[n][:], v), w=[n])
-
-    late = [
-        lambda: op("V", ts(T.jt[:], T.jt[:], mcol, ALU.add), r=["jt", "pm"], w=["jt"]),
-        lambda: op("V", ms(T.cr1[:], 160.0), w=["cr1"]),
-        lambda: op("V", ts(T.jk[:], T.jt[:], 1.0 / 33, ALU.mult, -0.485, ALU.add), r=["jt"], w=["jk"]),
-        lambda: op("V", tt(T.ccs[:], T.ccs[:], T.jt[:], ALU.add), r=["cc0", "cc1", "jt"], w=["ccs"]),
-        lambda: op("V", cp(T.jk32[:], T.jk[:]), r=["jk"], w=["jk32"]),
-        lambda: op("V", ms(T.cr2[:], 224.0), w=["cr2"]),
-        lambda: op("V", ts(T.jk[:], T.jk32[:], 3.0, ALU.min), r=["jk32"], w=["jk"]),
-        lambda: op("V", ts(T.jt[:], T.jk32[:], -33.0, ALU.mult), r=["jk32"], w=["jt"]),
-        lambda: op("V", tt(T.kp[:], T.jk[:], T.kp0[:], ALU.mult), r=["jk", "kq0", "kq1", "kq2"], w=["kp"]),
-        lambda: op("V", tt(T.ccs[:], T.ccs[:], T.jt[:], ALU.add), r=["ccs", "jt"], w=["ccs"]),
-        lambda: op("V", ts(T.ccs[:], T.ccs[:], 8.0, ALU.mult), r=["ccs"], w=["ccs"]),
-        lambda: op("V", cp(T.y1[:], T.ccs[:]), r=["ccs"], w=["y1"])]
+    jts = ["jt0", "jt1", "jt2"]
+    op("V", ts(T.jk[:], T.jt[:], 1.0 / 33, ALU.mult, -0.485, ALU.add), r=jts, w=["jk"])
+    op("V", tt(T.ccs[:], T.ccs[:], T.jt[:], ALU.add), r=["cc0", "cc1"] + jts, w=["ccs"])
+    op("V", cp(T.jk32[:], T.jk[:]), r=["jk"], w=["jk32"])
+    op("V", ms(T.c32[:], 32.0), w=["c32"])
+    op("V", ts(T.jk[:], T.jk32[:], 3.0, ALU.min), r=["jk32"], w=["jk"])
+    op("V", ts(T.jt[:], T.jk32[:], -33.0, ALU.mult), r=["jk32"], w=jts)
+    op("V", tt(T.kp[:], T.jk[:], T.kp0[:], ALU.mult), r=["jk", "kq0", "kq1", "kq2"], w=["kp"])
+    op("V", tt(T.ccs[:], T.ccs[:], T.jt[:], ALU.add), r=["ccs"] + jts, w=["ccs"])
+    op("V", ms(T.cr0[:], 96.0), w=["cr0"])
+    op("V", ts(T.ccs[:], T.ccs[:], 8.0, ALU.mult), r=["ccs"], w=["ccs"])
+    op("V", ms(T.c512[:], 512.0), w=["c512"])
+    op("V", cp(T.y1[:], T.ccs[:]), r=["ccs"], w=["y1"])
+    late = [lambda n=n, v=v: op("V", ms(T[n][:], v), w=[n])
+            for n, v in (("diff", 0.0), ("zero", 0.0), ("ones", 1.0), ("cr1", 160.0), ("cr2", 224.0))]
 
     psS = [T.psS0, T.psS1]
-    srows = [[k for k in SORD if k not in VROWS[c]] for c in range(NC)]
+    vrows = [VR0, VROWS, VROWS]
+    srows = [[[k for k in SORD if k not in vrows[t][c]] for c in range(NC)] for t in range(RO)]
 
     def zcopy(t, c):
         c0, c1 = CH[c]
         lz = "lz%d" % t
-        for k, e in zip(srows[c], ZENG[t][c]):
+        for k, e in zip(srows[t][c], ZENG[t][c]):
             o, i = row(T.B1, c0, c1, k + 1), T[lz][:, 16 * c0:16 * c1]
             if e == "S":
                 fn = act(o, i, ACT.Copy)
@@ -235,31 +245,31 @@ def rank_program(g, core, T, topo):
                 fn = cp(o, i)
             else:
                 fn = lambda o=o, i=i: g.affine_select(o, i, [[0, 16 * (c1 - c0)]], ALU.is_ge, 0.0, 0, 0)
-            op(e, fn, r=[lz], w=["z%d_%d" % (c, k)])
+            op(e, fn, r=["%s_%d" % (lz, c)], w=["z%d_%d" % (c, k)])
 
     def off(k, c):
         c0, c1 = CH[c]
         o = T.off2 if k & 1 else T.off1
         return T.X[:, 0:4096].indirect(o[:, 32 * (k >> 1) + c0:32 * (k >> 1) + c1]), ("off2" if k & 1 else "off1")
 
-    def sgather(c):
+    def sgather(t, c):
         c0, c1 = CH[c]
-        for k in srows[c]:
+        for k in srows[t][c]:
             w, tag = off(k, c)
             op("S", act(row(T.B0, c0, c1, k + 1), w, ACT.Copy), r=[tag, "X0", "X1"], w=["x%d_%d" % (c, k)])
 
     def vgather(t, c):
         c0, c1 = CH[c]
         lz = "lz%d" % t
-        for k in VROWS[c]:
+        for k in vrows[t][c]:
             w, tag = off(k, c)
-            op("V", tt(row(T.B0, c0, c1, k + 1), w, T[lz][:, 16 * c0:16 * c1], ALU.min), r=[tag, "X0", "X1", lz], w=["x%d_%d" % (c, k)])
+            op("V", tt(row(T.B0, c0, c1, k + 1), w, T[lz][:, 16 * c0:16 * c1], ALU.min), r=[tag, "X0", "X1", "%s_%d" % (lz, c)], w=["x%d_%d" % (c, k)])
 
     def scan(t, c):
         c0, c1 = CH[c]
         for m in range(16):
             op("V", scn(lane(T.TOP, c0, c1, m), lane(T.B0, c0, c1, m), lane(T.B1, c0, c1, m), 0.0, ALU.max, ALU.min),
-               r=["x%d_%d" % (c, k) for k in range(8)] + ["z%d_%d" % (c, k) for k in srows[c]] + ["k%d_%d" % (c, k) for k in VROWS[c]] + ["s0a", "s0b"],
+               r=["x%d_%d" % (c, k) for k in range(8)] + ["z%d_%d" % (c, k) for k in range(8)] + ["s0a", "s0b"],
                w=["top%d_%d" % (c, m)])
             op("T", mms([(psS[c][:, 0:c1 - c0, 0:9], T.mst[:, 15 - m:143 - m], lane(T.TOP, c0, c1, m), m == 0, m == 15)]),
                r=["top%d_%d" % (c, m), "mst"], w=["S%d" % c], x=["bS%d" % c])
@@ -274,13 +284,14 @@ def rank_program(g, core, T, topo):
     def zabs(t, c):
         a, b = 16 * CH[c][0], 16 * CH[c][1]
         op("S", act(T["zn%d" % t][:, a:b], T.psZ[:, a:b], ACT.Abs, bias=255.0, scale=-1.0), r=["Z%d" % c], w=["zn%d_%d" % (t, c)], x=["bZ"])
+        sendz(T["zn%d" % t], ["zn%d_%d" % (t, c)], q - RO if t == RO - 1 else q + 1, t + 1, c)
 
     def zmm(t, c):
         c0, c1 = CH[c]
         lz = "lz%d" % t
         o = T.psZ[:, 16 * c0:16 * c1]
         op("T", mms([(o, T.idb[:], T[lz][:, 16 * c0:16 * c1], True, False), (o, T.idb[:], row(T.TOP, c0, c1, 8), False, True)]),
-           r=["top%d_%d" % (c, m) for m in range(16)] + ["idb", lz], w=["Z%d" % c], x=["bZ"])
+           r=["top%d_%d" % (c, m) for m in range(16)] + ["idb", "%s_%d" % (lz, c)], w=["Z%d" % c], x=["bZ"])
 
     def prevt(c):
         c0, c1 = CH[c]
@@ -306,19 +317,24 @@ def rank_program(g, core, T, topo):
     def unroll(t, h):
         gu, u01, ro = T["gu%d" % h], T["u01%d" % (t & 1)], T["ro%d" % t]
         o = T.psR[:, 4 * h:4 * h + 4, 0:33]
-        op("T", mms([(o, T.cm32[:], T.c512[:, 0:132], True, False)]), r=["cm32", "c512"], w=["R%d" % h], x=["bR"])
-        op("V", tt(gu[:], T.LV[:, 4 * LS * h:4 * LS * (h + 1)].indirect(ro[:, 10:19]), T.rq[:], ALU.subtract),
-           r=["L%d" % (4 * h + j) for j in range(4)] + ["ro%d" % t, "rq"], w=["gu%d" % h])
-        op("T", mms([(o, u01[:, 0:128], gu[:, 1:133], False, t == 0), (o, u01[:, 128:256], gu[:, 0:132], False, True)][:2 if t else 1]),
+        win = T.LV[:, 4 * LS * h:4 * LS * (h + 1)].indirect(ro[:, 10:19])
+        lv = ["L%d" % (4 * h + j) for j in range(4)] + ["ro%d" % t]
+        ons = h == 0 or t == RO - 1
+        if ons:
+            op("T", mms([(o, u01[:, 0:128], T.nrq[:, 1:133], True, False), (o, u01[:, 128:256], T.nrq[:, 0:132], False, False)][:2 if t else 1]),
+               r=["nrq", "u01%d" % (t & 1)], w=["R%d" % h], x=["bR"])
+            op("S", act(gu[:], win, ACT.Copy), r=lv, w=["gu%d" % h])
+        else:
+            op("V", tt(gu[:], win, T.nrq[:], ALU.add), r=lv + ["nrq"], w=["gu%d" % h])
+        op("T", mms([(o, u01[:, 0:128], gu[:, 1:133], not ons, t == 0), (o, u01[:, 128:256], gu[:, 0:132], False, True)][:2 if t else 1]),
            r=["gu%d" % h, "u01%d" % (t & 1)], w=["R%d" % h], x=["bR"])
 
     def upper(t):
         Q = T["Q%d" % t]
         old, tag = (T.zero[:], "zero") if t == 0 else (T["Q%d" % (t - 1)][:, 128:256], "Q%d_hi" % (t - 1))
         st = [lambda: level(t, 4), lambda: level(t, 5), lambda: pp(t, 4), lambda: level(t, 6), lambda: pp(t, 5), lambda: level(t, 7),
-              lambda: pp(t, 6), lambda: pp(t, 7)]
+              lambda: unroll(t, 1), lambda: pp(t, 6), lambda: pp(t, 7)]
         st.append(lambda: send(T["P%d" % t][:, 128:256], ["P%d_%d" % (t, j) for j in range(4, 8)], [(q - t - 1, "lu_%d" % t if t < RO - 1 else "lP1")]))
-        st.append(lambda: unroll(t, 1))
         st.append(lambda: op("V", tt(Q[:, 128:256], T.psR[:, 4:8, 0:32], old, ALU.max), r=["R1", tag], w=["Q%d_hi" % t], x=["bR"]))
         return st
 
@@ -343,11 +359,12 @@ def rank_program(g, core, T, topo):
               lambda: op("S", act(u01[:], T.ua[:], ACT.Relu, bias=1.0, scale=-1.0), r=["ua"], w=["u01%d" % (t & 1)])]
         return st
 
-    up = late + turn(0)[9:13]
+    st = turn(0)
+    for s in (st[9], late[0], st[10], late[1], st[12], late[2]):
+        s()
+    up, gap = [], late[3:]
     for c in range(NC):
         zcopy(0, c)
-    op("G", iota(T.LV[:, 0:4 * LS], [[0, 4 * LS]], 16000000, 0), w=["lv0"])
-    op("G", iota(T.LV[:, 4 * LS:8 * LS], [[0, 4 * LS]], 16000000, 0), w=["lv1"])
     op("G", iota(T.e1[:], [[-16, 3], [-80, 8], [-1, 16]], 16, 1), w=["e1"])
 
     for t in range(RO):
@@ -358,11 +375,10 @@ def rank_program(g, core, T, topo):
         psK = T["ps" + kt]
         kgrp = [(psK[:, 0:256], T.c32[:], T.kb[:], True, False), (psK[:, 0:256], T["cr%d" % t][:], T.c512[:], False, False)]
         if t == 0:
-            op("V", cp(T.off2[:], T.a2[:]), r=["a2"], w=["off2"])
-            op("V", cp(T.off1[:], T.a1[:]), r=["a1"], w=["off1"])
-            op("V", ts(T.a2h[:], T.a2[:], -2048.0, ALU.add), r=["a2"], w=["a2h"])
-            op("V", ts(T.a1h[:], T.a1[:], -2048.0, ALU.add), r=["a1"], w=["a1h"])
             op("V", ms(T.a2[:, 96:128], 0.0), w=["a2"])
+            op("V", ts(T.a2h[:], T.off2[:], -2048.0, ALU.add), r=["off2"], w=["a2h"])
+            op("V", cp(T.a2[:, 0:96], T.off2[:, 0:96]), r=["off2"], w=["a2"])
+            op("V", ts(T.a1h[:], T.off1[:], -2048.0, ALU.add), r=["off1"], w=["a1h"])
             ap, aptag = T.a2, "a2"
             kgrp += [(psK[:, 2 * k + 1:256:8], T.idb[:], T.a2h[:, 32 * k:32 * k + 32], False, False) for k in range(4)]
             ktags = ["a2h"]
@@ -376,14 +392,19 @@ def rank_program(g, core, T, topo):
             o = T.psR[:, 0:4, 0:33]
             op("T", mms([(o, T.p01[:, 128:256], T.gr[:, 0:132], True, False), (o, T.p01[:, 0:128], T.gr[:, 1:133], False, True)]),
                r=["gr", "p01"], w=["R0"], x=["bR"])
-            if up:
-                up.pop(0)()
+            up[0]()
             op("V", ts(T.off2[:], T.psR[:, 0:4, 0:32], 2048.0, ALU.add), r=["R0"], w=["off2"], x=["bR"])
+            up[1]()
+            up[2]()
+            up[3]()
             op("V", tt(T.m1[:], T["lp1_%d" % p][:], T["lq_%d" % p][:], ALU.max), r=["lp1_%d" % p, "lq_%d" % p], w=["m1"])
             op("G", lambda: g.iota(T.a2c[:, 96:128], [[0, 32]], 0, 0), w=["a2c"])
+            up[4]()
             op("V", ts(T.a1c[:], T.m1[:], 4095, ALU.bitwise_and), r=["m1"], w=["a1c"])
+            up[7]()
+            op("V", cp(T.off1[:], T.a1c[:]), r=["a1c"], w=["off1"])
             op("V", ts(T.a1h[:], T.a1c[:], -2048.0, ALU.add), r=["a1c"], w=["a1h"])
-            op("V", ts(T.off1[:], T.a1h[:], 2048.0, ALU.add), r=["a1h"], w=["off1"])
+            up, gap = [up[5], up[6], up[8], up[9]], [up[10]]
             ap, aptag = T.a2c, "a2c"
             for k in range(4):
                 kgrp += [(psK[:, 2 * k + 1:256:8], T.p01[:, 128:256], T.gr[:, 33 * k:33 * k + 32], False, False),
@@ -393,7 +414,9 @@ def rank_program(g, core, T, topo):
         op("T", mms(kgrp), r=ktags + ["a1h", "idb", "c32", "kb0", "kb1", "c512", "cr%d" % t], w=[kt], x=["b" + kt])
 
         for c in range(NC):
-            sgather(c)
+            sgather(t, c)
+        if t:
+            up.pop(0)()
         for c in range(NC):
             vgather(t, c)
         n1 = UP1 if t else 8
@@ -411,15 +434,19 @@ def rank_program(g, core, T, topo):
         prevt(NC - 1)
         zmm(t, NC - 1)
         vmm(0)
-        for c in range(NC):
-            click(c)
+        click(0)
+        for s in gap:
+            s()
+        if last:
+            op("V", tt(T.U[:], T.lu_0[:], T.A8[:, 128:256], ALU.max), r=["lu_0"] + ["A8_%d" % j for j in range(4, 8)], w=["U"])
+        click(1)
         op("T", mms([(psK[:, 0:256], T.idn[:], T.click[:], False, True)]), r=clicks + ["idn"], w=[kt], x=["b" + kt])
         vmm(1)
         zabs(t, NC - 1)
-        send(T["zn%d" % t][:], ["zn%d_%d" % (t, c) for c in range(NC)], [(q - d if last else q + 1, "lz%d" % (t + 1))])
         op("V", scn(T.diff[:, 8:264], T.dmask[:], T.click[:], 0.0, ALU.mult, ALU.add), r=clicks + ["dmask"], w=["diff"])
         op("S", act(T.rp[:], T.diff[:, 15:264:8], ACT.Relu, bias=BIG, scale=-BIG), r=["diff"], w=["rp"])
         op("S", act(T.rq[:], T.diff[:, 0:288].indirect(ro[:, 20:29]), ACT.Relu, bias=BIG, scale=BIG), r=["diff", "ro%d" % t], w=["rq"])
+        op("S", act(T.nrq[:], T.rq[:], ACT.Identity, bias=-KK, scale=-1.0), r=["rq"], w=["nrq"])
         if not last:
             op("S", act(T.junk[:], T.click[:], ACT.Identity, accum_out=T.cnt[:, 0:1]), r=clicks, w=["cnt", "junk"])
             op("T", mms([(T.psC[:, 0:1], T.ones[:], T.cnt[:, 0:1], True, True)]), r=["ones", "cnt"], w=["tot"], x=["bC"])
@@ -432,12 +459,12 @@ def rank_program(g, core, T, topo):
         op("S", act(T.sq[:], T.uf[:], ACT.Square, bias=2.0, scale=0.25), r=["uf"], w=["sq"])
         op("S", act(T.hf[:], T.sq[:], ACT.Identity, bias=-4.25), r=["sq"], w=["hf"])
         level(t, 3)
+        unroll(t, 0)
         pp(t, 0)
         pp(t, 3)
         pp(t, 1)
         pp(t, 2)
         op("V", tt(P[:, 96:128], P[:, 96:128], T.hf[:], ALU.max), r=["P%d_3" % t, "hf"], w=["P%d_3" % t])
-        unroll(t, 0)
         qlo = lambda: op("V", tt(Q[:, 0:128], T.psR[:, 0:4, 0:32], ap[:], ALU.max), r=["R0", aptag], w=["Q%d_lo" % t], x=["bR"])
         if not last:
             send2(P[:, 0:128], ["P%d_%d" % (t, j) for j in range(4)], [(q - d - 1, "lp2_%d" % t), (q + 1, "lp1_%d" % t)])
@@ -452,18 +479,15 @@ def rank_program(g, core, T, topo):
             for s in st[2:8]:
                 s()
             for h in range(2):
-                st[8 + h]()
                 op("V", cp(T.X[:, 2048 * h:2048 * h + 2048].indirect(T.pl[:, 16 * h:16 * h + 16]), row(T.TOP, 16 * h, 16 * h + 16, 8)),
                    r=tops + ["pl"], w=["X%d" % h])
+                st[8 + h]()
+            up = upper(t)
             st[10]()
             zcopy(t + 1, 0)
             for s in st[13:]:
                 s()
             fin = st[11:13]
-            up = upper(t)
-            for s in up[:UPW]:
-                s()
-            up = up[UPW:]
             for c in range(1, NC):
                 zcopy(t + 1, c)
         else:
@@ -474,9 +498,8 @@ def rank_program(g, core, T, topo):
                 s()
             send(Q[:, 128:256], ["Q2_hi"], [(q + 1, "lQ1")])
 
-    op("S", act(T.zout[:], T.lz3[:], ACT.Copy), r=["lz3"], w=["zout"])
+    op("S", act(T.zout[:], T.lz3[:], ACT.Copy), r=["lz3_0", "lz3_1"], w=["zout"])
     dma("S", T.yz[:], T.zout[:], "dyz", r=["zout"])
-    op("V", tt(T.U[:], T.lu_0[:], T.A8[:, 128:256], ALU.max), r=["lu_0"] + ["A8_%d" % j for j in range(4, 8)], w=["U"])
     op("V", tt(T.U[:], T.lu_1[:], T.U[:], ALU.max), r=["lu_1", "U"], w=["U"])
     for h in range(2):
         b = slice(128 * h, 128 * h + 128)

from concourse.bass import DstId, RemoteDMATransfer
from concourse.mybir import AluOpType as ALU, ActivationFunctionType as ACT

N, RO = 8, 3
KK = float(2 ** 21)
BIG = float(2 ** 24)
CH = [(0, 18), (18, 32)]
VR0 = [(0, 2, 4), (0, 2, 4)]
VROWS = [(0, 2), (0, 2)]
SORD = (1, 3, 5, 7, 0, 2, 4, 6)
ZENG = [["SVSVSVSV", "GGGGGGGG"], ["SSGSGSSS", "GGGGGGGG"], ["SSGSGSSS", "GGGGGGGG"]]
NC = len(CH)
UP1, PSPLIT = 3, 1
LS = 264

F, BF, I32, U16, F16 = "float32", "bfloat16", "int32", "uint16", "float16"
SCRATCH = {}
for _dt, _lst in (
        (BF, dict(X=4096, B0=4736, B1=4736, TOP=4736, zin=512, mst=144, wmst=144, idb=128, idn=128, kb=256, c32=128,
                  cr0=128, cr1=128, cr2=128, c512=256, dmask=256, click=256, junk=256, diff=288, ua=256, lz0=512, lz1=512, lz2=512, lz3=512,
                  zn0=512, zn1=512, zn2=512)),
        (F, dict(raf=256, A8=256, wtf=8, zout=512, a2=128, ix=256, pcf=4, e1=384, ones=128, i8=32, jt=30, jk=30, ccs=30,
                 kp=30, kp0=30, sgn=30, gu0=144, gu1=144, u010=256, u011=256, rp=32, rq=144, nrq=144, LV=8 * LS, uf=32, sq=32, hf=32, cnt=4, tf=4, y0=30,
                 U=128, ff=256, Y=256, lP0=128, lQ0=128, lP1=128, lQ1=128, P0=256, P1=256, P2=256, Q0=256, Q1=256, Q2=256, zero=128,
                 lp1_0=128, lp2_0=128, lq_0=128, lu_0=128, lp1_1=128, lp2_1=128, lq_1=128, lu_1=128)),
        (I32, dict(ra32=256, wt32=8, pc32=4, jk32=30, m1=128, m2=128, a1c=128, a2c=128, v32=32, u32=32, u7=32, pl32=32, t32=4,
                   y1=30, y2=30, y3=30, f32=256, f33=256)),
        (U16, dict(off1=128, off2=128, a16=128, pl=32, ro0=30, ro1=30, ro2=30)),
        (BF, dict(p01=256)), (F16, dict(a1h=128, a2h=128, gr=144))):
    for _n, _c in _lst.items():
        SCRATCH[_n] = ("sbuf", [128, _c], _dt)
SCRATCH["tr"] = ("sbuf", [128, 2, 8, 2, 8], F)
SCRATCH["prev"] = ("sbuf", [128, 32, 8], F)
for _n, _s in (("psS0", [32, 16]), ("psS1", [32, 16]), ("psZ", [512]), ("psV", [512]), ("psK0", [512]), ("psK1", [512]),
               ("psR", [8, 64]), ("psC", [512])):
    SCRATCH[_n] = ("psum", [128] + _s, F)

ARR = ["off1", "off2", "lP0", "lQ0", "lP1", "lQ1"] + ["lz%d_%d" % (t, c) for t in range(RO + 1) for c in range(NC)] + ["%s%d" % (n, t) for t in range(RO - 1) for n in ("lp1_", "lp2_", "lq_", "lu_")]
SEMAPHORES = ["cV", "cS", "cT", "cG", "sent", "dra", "dzu", "dw", "dt", "dx0", "dx1", "dya", "dyz"] + ["r_" + a for a in ARR]


def rank_program(g, core, T, topo):
    q = T.rank_of(core)
    if q is None:
        return
    cores = T.cores
    V, S, PE = g.vector, g.scalar, g.tensor
    eng = {"V": V, "S": S, "T": PE, "G": g, "Y": g.sync}
    mask = -1
    for a in cores:
        for b in cores:
            if a != b:
                mask &= topo.mask(a, b)
    bits = [b for b in range(mask.bit_length()) if mask >> b & 1]
    neng = len(bits)

    writer, readers, bank, total = {}, {}, {}, {}
    seen = {e: {} for e in eng}
    for a in ARR:
        n = neng // 2 if not PSPLIT and (a in ("off1", "off2") or a.startswith("lp")) else neng
        writer[a] = ("r_" + a, n)
        total["r_" + a] = n

    def waits(e, r, w, x):
        need = {}
        evs = [writer[t] for t in r]
        for t in w:
            evs += [ev for ev in [writer.get(t)] + readers.get(t, []) if ev is not None and not (e == "T" and ev[0] == "cT")]
        evs += [bank[t] for t in x if t in bank and bank[t][0] != "c" + e]
        for s, n in evs:
            need[s] = max(need.get(s, 0), n)
        for s, n in need.items():
            if seen[e].get(s, 0) < n:
                eng[e].wait_ge(T.sem[s], n)
                seen[e][s] = n

    def note(ev, r, w, x):
        for t in r:
            readers.setdefault(t, []).append(ev)
        for t in w:
            writer[t] = ev
            readers[t] = []
        for t in x:
            bank[t] = ev

    def op(e, fn, r=(), w=(), x=()):
        waits(e, r, w, x)
        s = "c" + e
        total[s] = total.get(s, 0) + 1
        fn().then_inc(T.sem[s], 1)
        note((s, total[s]), r, w, x)

    def dma(e, out, in_, s, r=(), w=()):
        waits(e, r, w, ())
        eng[e].dma_start(out, in_).then_inc(T.sem[s], 16)
        total[s] = 16
        note((s, 16), r, w, ())

    def send(src, r, dsts, dst=None):
        waits("G", r, (), ())
        trs = []
        n = len(dsts)
        for j, (d, name) in enumerate(dsts):
            rid, pid = topo.addr(cores[d % N], core)
            m = 0
            for b in bits[j * neng // n:(j + 1) * neng // n]:
                m |= 1 << b
            trs.append(RemoteDMATransfer(dst_ids=[DstId(rid=rid, pnc=pid)], dma_engine_mask=m, remote_sem=T.sem["r_" + name],
                                         src=src, dsts=[T[name][:] if dst is None else dst]))
        g.remote_dma_fused(trs, local_sem=T.sem.sent)
        total["sent"] = total.get("sent", 0) + neng

    def sendz(src, r, d, t, c):
        a, b = 16 * CH[c][0], 16 * CH[c][1]
        send(src[:, a:b], r, [(d, "lz%d_%d" % (t, c))], T["lz%d" % t][:, a:b])

    def send2(src, r, dsts):
        if PSPLIT:
            for x in dsts:
                send(src, r, [x])
        else:
            send(src, r, dsts)

    def ts(out, in0, s1, o0, s2=None, o1=None):
        if o1 is None:
            return lambda: V.tensor_scalar(out, in0, s1, None, o0)
        return lambda: V.tensor_scalar(out, in0, s1, s2, o0, o1)

    def tt(out, a, b, o):
        return lambda: V.tensor_tensor(out, a, b, o)

    def cp(out, a):
        return lambda: V.tensor_copy(out, a)

    def ms(out, v):
        return lambda: V.memset(out, v)

    def act(out, a, f, **kw):
        return lambda: S.activation(out, a, f, **kw)

    def scn(out, a, b, init, o0, o1):
        return lambda: V.tensor_tensor_scan(out, a, b, init, o0, o1)

    def mms(lst):
        def f():
            ins = None
            for o, l, rr, a, b in lst:
                ins = PE.matmul(o, l, rr, a, b)
            return ins
        return f

    def iota(out, pat, base, cm):
        return lambda: g.iota(out, pat, base, cm, allow_small_or_imprecise_dtypes=True)

    def row(buf, c0, c1, s):
        a = 144 * c0 + 16 * s
        return buf[:, a:a + 9 * (16 * (c1 - c0) - 1) + 1:9]

    def lane(buf, c0, c1, m):
        a = 144 * c0 + 9 * m
        return buf[:, a:a + 16 * (9 * (c1 - c0) - 1) + 1:16]

    dma("Y", T.ra32[:], T.ra[:], "dra", w=["ra32"])
    dma("S", T.zin[:], T.zu[:], "dzu", w=["zin"])
    dma("Y", T.X[:, 0:2048], T.xd[:, 0:2048], "dx0", w=["X0"])
    dma("S", T.X[:, 2048:4096], T.xd[:, 2048:4096], "dx1", w=["X1"])
    dma("Y", T.wt32[:, 0:1], T.wg[:], "dw", w=["wg"])
    dma("Y", T.wt32[:, 4:5], T.th[:], "dt", w=["th"])

    op("G", iota(T.ix[:], [[1, 256]], 0, 0), w=["ix"])
    op("G", lambda: g.iota(T.pc32[:, 0:1], [[0, 1]], 0, 1), w=["p32"])
    op("G", iota(T.kb[0:64, :], [[-32, 32], [0, 8]], 0, 0), w=["kb0"])
    op("G", iota(T.kb[64:128, :], [[0, 32], [2, 8]], -15, 0), r=["ix", "p32", "kb0"], w=["kb1"])
    op("V", ms(row(T.B0, 0, 32, 0), 0.0), w=["s0a"])
    op("V", ms(row(T.B1, 0, 32, 0), 0.0), w=["s0b"])
    for c, (c0, c1) in enumerate(CH):
        for k in VR0[c]:
            op("V", ms(row(T.B1, c0, c1, k + 1), 255.0), w=["z%d_%d" % (c, k)])
    op("V", ms(T.dmask[:], -1.0), w=["dmask"])
    op("V", ts(T.pc32[:, 1:2], T.pc32[:, 0:1], 15, ALU.bitwise_and), r=["p32"], w=["m32"])
    op("V", ms(T.dmask[:, 0:256:8], 0.0), w=["dmask"])
    op("V", cp(T.pcf[:, 0:2], T.pc32[:, 0:2]), r=["p32", "m32"], w=["pm"])
    pcol, mcol, gcol, m8 = T.pcf[:, 0:1], T.pcf[:, 1:2], T.pcf[:, 2:3], T.pcf[:, 3:4]
    op("V", tt(gcol, pcol, mcol, ALU.subtract), r=["pm"], w=["gcol"])
    op("V", ts(m8, mcol, 8.0, ALU.mult), r=["pm"], w=["m8"])

    sendz(T.zin, ["zin"], q + 1, 0, 0)
    op("V", cp(T.raf[:], T.ra32[:]), r=["ra32"], w=["raf"])
    for e in range(8):
        op("V", lambda e=e: V.transpose(T.tr[:, :, e], T.raf[:, e:256:8]), r=["raf"], w=["tr%d" % e])
    trs8 = ["tr%d" % e for e in range(8)]
    for k in range(8):
        op("V", lambda k=k: V.transpose(T.A8[:, 32 * k:32 * k + 32], T.tr[:, :, :, :, k]), r=trs8, w=["A8_%d" % k])
        if k == 3:
            op("V", cp(T.a16[:], T.A8[:, 0:128]), r=["A8_%d" % j for j in range(4)], w=["a16"])
            send2(T.a16[:], ["a16"], [(q - 1, "off2"), (q + 1, "off1")])
            sendz(T.zin, ["zin"], q + 1, 0, 1)
    op("G", iota(T.LV[:, 0:4 * LS], [[0, 4 * LS]], 16000000, 0), r=["kb1"], w=["lv0"])
    op("G", iota(T.LV[:, 4 * LS:8 * LS], [[0, 4 * LS]], 16000000, 0), w=["lv1"])
    for j in range(3):
        op("S", act(T.jt[:, 10 * j:10 * j + 10], T.ix[:, 0:10], ACT.Identity, scale=16.0, bias=mcol), r=["ix", "pm"], w=["jt%d" % j])
    for n, a, b, v, tag in (("sgn", 0, 10, 1, "sg0"), ("sgn", 10, 30, -1, "sg1"), ("ccs", 0, 10, 0, "cc0"), ("ccs", 10, 30, 4127, "cc1"),
                            ("kp0", 0, 10, 256, "kq0"), ("kp0", 10, 20, LS, "kq1"), ("kp0", 20, 30, 0, "kq2")):
        op("V", ms(T[n][:, a:b], float(v)), w=[tag])
    op("V", ts(T.mst[:], T.ix[:, 0:144], gcol, ALU.subtract, 15.0, ALU.is_equal), r=["ix", "gcol"], w=["mst"])
    op("V", cp(T.wtf[:, 0:1], T.wt32[:, 0:1]), r=["wg"], w=["wf"])
    op("V", cp(T.wtf[:, 4:5], T.wt32[:, 4:5]), r=["th"], w=["tf0"])
    wcol, tcol = T.wtf[:, 0:1], T.wtf[:, 4:5]
    op("V", ts(T.idb[:], T.ix[:, 0:128], pcol, ALU.is_equal), r=["ix", "pm"], w=["idb"])
    op("S", act(T.wmst[:], T.mst[:], ACT.Copy, scale=wcol), r=["mst", "wf"], w=["wmst"])
    op("S", act(T.idn[:], T.idb[:], ACT.Copy, scale=-32768.0), r=["idb"], w=["idn"])
    for h in range(2):
        op("S", act(T.i8[:, 16 * h:16 * h + 16], T.ix[:, 0:16], ACT.Identity, scale=128.0, bias=m8), r=["ix", "m8"], w=["i8"])
    op("S", act(T.u010[:, 0:128], T.idb[:], ACT.Copy), r=["idb"], w=["u010"])
    g4 = T.wtf[:, 1:2]
    op("S", act(g4, gcol, ACT.Copy, scale=4.0), r=["gcol"], w=["g4"])
    jts = ["jt0", "jt1", "jt2"]
    op("V", ts(T.jk[:], T.jt[:], 1.0 / 33, ALU.mult, -0.485, ALU.add), r=jts, w=["jk"])
    op("V", tt(T.ccs[:], T.ccs[:], T.jt[:], ALU.add), r=["cc0", "cc1"] + jts, w=["ccs"])
    op("V", cp(T.jk32[:], T.jk[:]), r=["jk"], w=["jk32"])
    op("V", ms(T.c32[:], 32.0), w=["c32"])
    op("V", ts(T.jk[:], T.jk32[:], 3.0, ALU.min), r=["jk32"], w=["jk"])
    op("V", ts(T.jt[:], T.jk32[:], -33.0, ALU.mult), r=["jk32"], w=jts)
    op("V", tt(T.kp[:], T.jk[:], T.kp0[:], ALU.mult), r=["jk", "kq0", "kq1", "kq2"], w=["kp"])
    op("V", tt(T.ccs[:], T.ccs[:], T.jt[:], ALU.add), r=["ccs"] + jts, w=["ccs"])
    op("V", ms(T.cr0[:], 96.0), w=["cr0"])
    op("V", ts(T.ccs[:], T.ccs[:], 8.0, ALU.mult), r=["ccs"], w=["ccs"])
    op("V", ms(T.c512[:], 512.0), w=["c512"])
    op("V", cp(T.y1[:], T.ccs[:]), r=["ccs"], w=["y1"])
    late = [lambda n=n, v=v: op("V", ms(T[n][:], v), w=[n])
            for n, v in (("diff", 0.0), ("zero", 0.0), ("ones", 1.0), ("cr1", 160.0), ("cr2", 224.0))]

    psS = [T.psS0, T.psS1]
    vrows = [VR0, VROWS, VROWS]
    srows = [[[k for k in SORD if k not in vrows[t][c]] for c in range(NC)] for t in range(RO)]

    def zcopy(t, c):
        c0, c1 = CH[c]
        lz = "lz%d" % t
        for k, e in zip(srows[t][c], ZENG[t][c]):
            o, i = row(T.B1, c0, c1, k + 1), T[lz][:, 16 * c0:16 * c1]
            if e == "S":
                fn = act(o, i, ACT.Copy)
            elif e == "V":
                fn = cp(o, i)
            else:
                fn = lambda o=o, i=i: g.affine_select(o, i, [[0, 16 * (c1 - c0)]], ALU.is_ge, 0.0, 0, 0)
            op(e, fn, r=["%s_%d" % (lz, c)], w=["z%d_%d" % (c, k)])

    def off(k, c):
        c0, c1 = CH[c]
        o = T.off2 if k & 1 else T.off1
        return T.X[:, 0:4096].indirect(o[:, 32 * (k >> 1) + c0:32 * (k >> 1) + c1]), ("off2" if k & 1 else "off1")

    def sgather(t, c):
        c0, c1 = CH[c]
        for k in srows[t][c]:
            w, tag = off(k, c)
            op("S", act(row(T.B0, c0, c1, k + 1), w, ACT.Copy), r=[tag, "X0", "X1"], w=["x%d_%d" % (c, k)])

    def vgather(t, c):
        c0, c1 = CH[c]
        lz = "lz%d" % t
        for k in vrows[t][c]:
            w, tag = off(k, c)
            op("V", tt(row(T.B0, c0, c1, k + 1), w, T[lz][:, 16 * c0:16 * c1], ALU.min), r=[tag, "X0", "X1", "%s_%d" % (lz, c)], w=["x%d_%d" % (c, k)])

    def scan(t, c):
        c0, c1 = CH[c]
        for m in range(16):
            op("V", scn(lane(T.TOP, c0, c1, m), lane(T.B0, c0, c1, m), lane(T.B1, c0, c1, m), 0.0, ALU.max, ALU.min),
               r=["x%d_%d" % (c, k) for k in range(8)] + ["z%d_%d" % (c, k) for k in range(8)] + ["s0a", "s0b"],
               w=["top%d_%d" % (c, m)])
            op("T", mms([(psS[c][:, 0:c1 - c0, 0:9], T.mst[:, 15 - m:143 - m], lane(T.TOP, c0, c1, m), m == 0, m == 15)]),
               r=["top%d_%d" % (c, m), "mst"], w=["S%d" % c], x=["bS%d" % c])

    tops = ["top%d_%d" % (c, m) for c in range(NC) for m in range(16)]
    clicks = ["click%d" % c for c in range(NC)]

    def vmm(h):
        op("T", mms([(T.psV[:, 0:32], T.wmst[:, 15 - m:143 - m], T.TOP[:, 128 + 9 * m:4736:144], m == 0, m == 15)
                     for m in (range(6), range(6, 16))[h]]), r=tops + ["wmst"], w=["v"], x=["bV"])

    def zabs(t, c):
        a, b = 16 * CH[c][0], 16 * CH[c][1]
        op("S", act(T["zn%d" % t][:, a:b], T.psZ[:, a:b], ACT.Abs, bias=255.0, scale=-1.0), r=["Z%d" % c], w=["zn%d_%d" % (t, c)], x=["bZ"])
        sendz(T["zn%d" % t], ["zn%d_%d" % (t, c)], q - RO if t == RO - 1 else q + 1, t + 1, c)

    def zmm(t, c):
        c0, c1 = CH[c]
        lz = "lz%d" % t
        o = T.psZ[:, 16 * c0:16 * c1]
        op("T", mms([(o, T.idb[:], T[lz][:, 16 * c0:16 * c1], True, False), (o, T.idb[:], row(T.TOP, c0, c1, 8), False, True)]),
           r=["top%d_%d" % (c, m) for m in range(16)] + ["idb", "%s_%d" % (lz, c)], w=["Z%d" % c], x=["bZ"])

    def prevt(c):
        c0, c1 = CH[c]
        op("S", act(T.prev[:, c0:c1, :], psS[c][:, 0:c1 - c0, 0:8], ACT.Identity, bias=tcol),
           r=["S%d" % c, "tf0"], w=["prev%d" % c], x=["bS%d" % c])

    def click(c):
        c0, c1 = CH[c]
        op("V", tt(T.click[:, 8 * c0:8 * c1], psS[c][:, 0:c1 - c0, 1:9], T.prev[:, c0:c1, :], ALU.is_ge),
           r=["S%d" % c, "prev%d" % c], w=["click%d" % c], x=["bS%d" % c])

    def level(t, j):
        k = "K%d" % (t & 1)
        a = LS * j + 8
        prev = T.ix[:] if j == 0 else T.LV[:, a - LS - 1:a - LS + 255]
        op("V", scn(T.LV[:, a:a + 256], T["ps" + k][:, 0:256], prev, BIG, ALU.min, ALU.max),
           r=[k, "ix" if j == 0 else "L%d" % (j - 1), "lv0" if j < 4 else "lv1"], w=["L%d" % j], x=["b" + k])

    def pp(t, j):
        a = LS * j + 15
        op("V", tt(T["P%d" % t][:, 32 * j:32 * j + 32], T.LV[:, a:a + 249:8], T.rp[:], ALU.subtract), r=["L%d" % j, "rp"], w=["P%d_%d" % (t, j)])

    def unroll(t, h):
        gu, u01, ro = T["gu%d" % h], T["u01%d" % (t & 1)], T["ro%d" % t]
        o = T.psR[:, 4 * h:4 * h + 4, 0:33]
        win = T.LV[:, 4 * LS * h:4 * LS * (h + 1)].indirect(ro[:, 10:19])
        lv = ["L%d" % (4 * h + j) for j in range(4)] + ["ro%d" % t]
        ons = h == 0 or t == RO - 1
        if ons:
            op("T", mms([(o, u01[:, 0:128], T.nrq[:, 1:133], True, False), (o, u01[:, 128:256], T.nrq[:, 0:132], False, False)][:2 if t else 1]),
               r=["nrq", "u01%d" % (t & 1)], w=["R%d" % h], x=["bR"])
            op("S", act(gu[:], win, ACT.Copy), r=lv, w=["gu%d" % h])
        else:
            op("V", tt(gu[:], win, T.nrq[:], ALU.add), r=lv + ["nrq"], w=["gu%d" % h])
        op("T", mms([(o, u01[:, 0:128], gu[:, 1:133], not ons, t == 0), (o, u01[:, 128:256], gu[:, 0:132], False, True)][:2 if t else 1]),
           r=["gu%d" % h, "u01%d" % (t & 1)], w=["R%d" % h], x=["bR"])

    def upper(t):
        Q = T["Q%d" % t]
        old, tag = (T.zero[:], "zero") if t == 0 else (T["Q%d" % (t - 1)][:, 128:256], "Q%d_hi" % (t - 1))
        st = [lambda: level(t, 4), lambda: level(t, 5), lambda: pp(t, 4), lambda: level(t, 6), lambda: pp(t, 5), lambda: level(t, 7),
              lambda: unroll(t, 1), lambda: pp(t, 6), lambda: pp(t, 7)]
        st.append(lambda: send(T["P%d" % t][:, 128:256], ["P%d_%d" % (t, j) for j in range(4, 8)], [(q - t - 1, "lu_%d" % t if t < RO - 1 else "lP1")]))
        st.append(lambda: op("V", tt(Q[:, 128:256], T.psR[:, 4:8, 0:32], old, ALU.max), r=["R1", tag], w=["Q%d_hi" % t], x=["bR"]))
        return st

    def turn(t):
        ro, u01 = T["ro%d" % t], T["u01%d" % (t & 1)]
        tot, ttag, x = T.psC[:, 0:1], "tot", ["bC"]
        st = [lambda: op("V", cp(T.t32[:, 0:1], tot), r=[ttag], w=["t32"], x=x),
              lambda: op("V", ts(T.t32[:, 1:2], T.t32[:, 0:1], 4, ALU.logical_shift_right), r=["t32"], w=["tc32"]),
              lambda: op("V", ts(T.tf[:, 0:1], T.t32[:, 1:2], 8.0, ALU.mult), r=["tc32"], w=["tc"]),
              lambda: op("S", act(T.y0[:], T.sgn[:], ACT.Copy, scale=T.tf[:, 0:1]), r=["sg0", "sg1", "tc"], w=["y0"]),
              lambda: op("V", ts(T.tf[:, 1:2], T.t32[:, 1:2], -16.0, ALU.mult, tot, ALU.add), r=["tc32", ttag], w=["tm"], x=x),
              lambda: op("S", act(T.tf[:, 3:4], T.tf[:, 1:2], ACT.Identity, bias=g4, scale=-1.0), r=["g4", "tm"], w=["tmn"]),
              lambda: op("S", act(T.ua[:], T.e1[:, 0:256], ACT.Abs, bias=T.tf[:, 3:4]), r=["e1", "tmn"], w=["ua"]),
              lambda: op("S", act(T.p01[:], T.ua[:], ACT.Relu, bias=1.0, scale=-1.0), r=["ua"], w=["p01"]),
              lambda: op("V", tt(T.y1[:], T.y0[:], T.ccs[:], ALU.add), r=["y0", "ccs"], w=["y1"]),
              lambda: op("V", ts(T.y2[:], T.y1[:], 248, ALU.bitwise_and), r=["y1"], w=["y2"]),
              lambda: op("V", tt(T.y3[:], T.y2[:], T.kp[:], ALU.add), r=["y2", "kp"], w=["y3"]),
              lambda: t > 0 and op("V", ts(ro[:, 0:10], T.y3[:, 0:10], 0.125, ALU.mult), r=["y3"], w=["rr%d" % t]),
              lambda: op("V", ts(ro[:, 10:30], T.y3[:, 10:30], 15.0, ALU.add), r=["y3"], w=["ro%d" % t]),
              lambda: op("S", act(T.tf[:, 2:3], T.tf[:, 1:2], ACT.Identity, bias=g4), r=["g4", "tm"], w=["tmg"]),
              lambda: op("S", act(T.ua[:], T.e1[:, 128:384], ACT.Abs, bias=T.tf[:, 2:3]), r=["e1", "tmg"], w=["ua"]),
              lambda: op("S", act(u01[:], T.ua[:], ACT.Relu, bias=1.0, scale=-1.0), r=["ua"], w=["u01%d" % (t & 1)])]
        return st

    st = turn(0)
    for s in (st[9], late[0], st[10], late[1], st[12], late[2]):
        s()
    up, gap = [], late[3:]
    for c in range(NC):
        zcopy(0, c)
    op("G", iota(T.e1[:], [[-16, 3], [-80, 8], [-1, 16]], 16, 1), w=["e1"])

    for t in range(RO):
        d = t + 1
        last = t == RO - 1
        P, Q, ro = T["P%d" % t], T["Q%d" % t], T["ro%d" % t]
        kt = "K%d" % (t & 1)
        psK = T["ps" + kt]
        kgrp = [(psK[:, 0:256], T.c32[:], T.kb[:], True, False), (psK[:, 0:256], T["cr%d" % t][:], T.c512[:], False, False)]
        if t == 0:
            op("V", ms(T.a2[:, 96:128], 0.0), w=["a2"])
            op("V", ts(T.a2h[:], T.off2[:], -2048.0, ALU.add), r=["off2"], w=["a2h"])
            op("V", cp(T.a2[:, 0:96], T.off2[:, 0:96]), r=["off2"], w=["a2"])
            op("V", ts(T.a1h[:], T.off1[:], -2048.0, ALU.add), r=["off1"], w=["a1h"])
            ap, aptag = T.a2, "a2"
            kgrp += [(psK[:, 2 * k + 1:256:8], T.idb[:], T.a2h[:, 32 * k:32 * k + 32], False, False) for k in range(4)]
            ktags = ["a2h"]
        else:
            p = t - 1
            op("V", tt(T.m2[:], T["lp2_%d" % p][:], T["Q%d" % p][:, 0:128], ALU.max), r=["lp2_%d" % p, "Q%d_lo" % p], w=["m2"])
            fin[0]()
            op("V", ts(T.a2c[:], T.m2[:], 4095, ALU.bitwise_and), r=["m2"], w=["a2c"])
            fin[1]()
            op("V", ts(T.gr[:], T.a2c[:, 0:128].indirect(ro[:, 0:9]), -2048.0, ALU.add), r=["a2c", "rr%d" % t], w=["gr"])
            o = T.psR[:, 0:4, 0:33]
            op("T", mms([(o, T.p01[:, 128:256], T.gr[:, 0:132], True, False), (o, T.p01[:, 0:128], T.gr[:, 1:133], False, True)]),
               r=["gr", "p01"], w=["R0"], x=["bR"])
            up[0]()
            op("V", ts(T.off2[:], T.psR[:, 0:4, 0:32], 2048.0, ALU.add), r=["R0"], w=["off2"], x=["bR"])
            up[1]()
            up[2]()
            up[3]()
            op("V", tt(T.m1[:], T["lp1_%d" % p][:], T["lq_%d" % p][:], ALU.max), r=["lp1_%d" % p, "lq_%d" % p], w=["m1"])
            op("G", lambda: g.iota(T.a2c[:, 96:128], [[0, 32]], 0, 0), w=["a2c"])
            up[4]()
            op("V", ts(T.a1c[:], T.m1[:], 4095, ALU.bitwise_and), r=["m1"], w=["a1c"])
            up[7]()
            op("V", cp(T.off1[:], T.a1c[:]), r=["a1c"], w=["off1"])
            op("V", ts(T.a1h[:], T.a1c[:], -2048.0, ALU.add), r=["a1c"], w=["a1h"])
            up, gap = [up[5], up[6], up[8], up[9]], [up[10]]
            ap, aptag = T.a2c, "a2c"
            for k in range(4):
                kgrp += [(psK[:, 2 * k + 1:256:8], T.p01[:, 128:256], T.gr[:, 33 * k:33 * k + 32], False, False),
                         (psK[:, 2 * k + 1:256:8], T.p01[:, 0:128], T.gr[:, 33 * k + 1:33 * k + 33], False, False)]
            ktags = ["gr", "p01"]
        kgrp += [(psK[:, 2 * k:256:8], T.idb[:], T.a1h[:, 32 * k:32 * k + 32], False, False) for k in range(4)]
        op("T", mms(kgrp), r=ktags + ["a1h", "idb", "c32", "kb0", "kb1", "c512", "cr%d" % t], w=[kt], x=["b" + kt])

        for c in range(NC):
            sgather(t, c)
        if t:
            up.pop(0)()
        for c in range(NC):
            vgather(t, c)
        n1 = UP1 if t else 8
        for s in up[:n1]:
            s()
        for c in range(NC):
            if c == NC - 1:
                for s in up[n1:]:
                    s()
            scan(t, c)
            if c < NC - 1:
                zmm(t, c)
                prevt(c)
                zabs(t, c)
        prevt(NC - 1)
        zmm(t, NC - 1)
        vmm(0)
        click(0)
        for s in gap:
            s()
        if last:
            op("V", tt(T.U[:], T.lu_0[:], T.A8[:, 128:256], ALU.max), r=["lu_0"] + ["A8_%d" % j for j in range(4, 8)], w=["U"])
        click(1)
        op("T", mms([(psK[:, 0:256], T.idn[:], T.click[:], False, True)]), r=clicks + ["idn"], w=[kt], x=["b" + kt])
        vmm(1)
        zabs(t, NC - 1)
        op("V", scn(T.diff[:, 8:264], T.dmask[:], T.click[:], 0.0, ALU.mult, ALU.add), r=clicks + ["dmask"], w=["diff"])
        op("S", act(T.rp[:], T.diff[:, 15:264:8], ACT.Relu, bias=BIG, scale=-BIG), r=["diff"], w=["rp"])
        op("S", act(T.rq[:], T.diff[:, 0:288].indirect(ro[:, 20:29]), ACT.Relu, bias=BIG, scale=BIG), r=["diff", "ro%d" % t], w=["rq"])
        op("S", act(T.nrq[:], T.rq[:], ACT.Identity, bias=-KK, scale=-1.0), r=["rq"], w=["nrq"])
        if not last:
            op("S", act(T.junk[:], T.click[:], ACT.Identity, accum_out=T.cnt[:, 0:1]), r=clicks, w=["cnt", "junk"])
            op("T", mms([(T.psC[:, 0:1], T.ones[:], T.cnt[:, 0:1], True, True)]), r=["ones", "cnt"], w=["tot"], x=["bC"])
        level(t, 0)
        op("V", cp(T.v32[:], T.psV[:, 0:32]), r=["v"], w=["v32"], x=["bV"])
        level(t, 1)
        op("V", ts(T.u32[:], T.v32[:], 4095, ALU.bitwise_and), r=["v32"], w=["u32"])
        level(t, 2)
        op("V", cp(T.uf[:], T.u32[:]), r=["u32"], w=["uf"])
        op("S", act(T.sq[:], T.uf[:], ACT.Square, bias=2.0, scale=0.25), r=["uf"], w=["sq"])
        op("S", act(T.hf[:], T.sq[:], ACT.Identity, bias=-4.25), r=["sq"], w=["hf"])
        level(t, 3)
        unroll(t, 0)
        pp(t, 0)
        pp(t, 3)
        pp(t, 1)
        pp(t, 2)
        op("V", tt(P[:, 96:128], P[:, 96:128], T.hf[:], ALU.max), r=["P%d_3" % t, "hf"], w=["P%d_3" % t])
        qlo = lambda: op("V", tt(Q[:, 0:128], T.psR[:, 0:4, 0:32], ap[:], ALU.max), r=["R0", aptag], w=["Q%d_lo" % t], x=["bR"])
        if not last:
            send2(P[:, 0:128], ["P%d_%d" % (t, j) for j in range(4)], [(q - d - 1, "lp2_%d" % t), (q + 1, "lp1_%d" % t)])
            st = turn(t + 1)
            op("V", ts(T.u7[:], T.v32[:], 7, ALU.bitwise_and), r=["v32"], w=["u7"])
            st[0]()
            op("V", tt(T.pl32[:], T.u7[:], T.i8[:], ALU.add), r=["u7", "i8"], w=["pl32"])
            st[1]()
            op("V", cp(T.pl[:], T.pl32[:]), r=["pl32"], w=["pl"])
            qlo()
            send(Q[:, 0:128], ["Q%d_lo" % t], [(q + d + 2, "lq_%d" % t)])
            for s in st[2:8]:
                s()
            for h in range(2):
                op("V", cp(T.X[:, 2048 * h:2048 * h + 2048].indirect(T.pl[:, 16 * h:16 * h + 16]), row(T.TOP, 16 * h, 16 * h + 16, 8)),
                   r=tops + ["pl"], w=["X%d" % h])
                st[8 + h]()
            up = upper(t)
            st[10]()
            zcopy(t + 1, 0)
            for s in st[13:]:
                s()
            fin = st[11:13]
            for c in range(1, NC):
                zcopy(t + 1, c)
        else:
            send(P[:, 0:128], ["P%d_%d" % (t, j) for j in range(4)], [(q - d, "lP0")])
            up = upper(t)
            up[2:2] = [qlo, lambda: send(Q[:, 0:128], ["Q2_lo"], [(q + 1, "lQ0")])]
            for s in up:
                s()
            send(Q[:, 128:256], ["Q2_hi"], [(q + 1, "lQ1")])

    op("S", act(T.zout[:], T.lz3[:], ACT.Copy), r=["lz3_0", "lz3_1"], w=["zout"])
    dma("S", T.yz[:], T.zout[:], "dyz", r=["zout"])
    op("V", tt(T.U[:], T.lu_1[:], T.U[:], ALU.max), r=["lu_1", "U"], w=["U"])
    for h in range(2):
        b = slice(128 * h, 128 * h + 128)
        if h == 1:
            op("V", tt(T.U[:], T.lP1[:], T.U[:], ALU.max), r=["lP1", "U"], w=["U"])
        op("V", tt(T.f32[:, b], T.U[:] if h else T.lP0[:], T["lQ%d" % h][:], ALU.max), r=["U" if h else "lP0", "lQ%d" % h], w=["f32_%d" % h])
        op("V", ts(T.f33[:, b], T.f32[:, b], 4095, ALU.bitwise_and), r=["f32_%d" % h], w=["f33_%d" % h])
        op("V", cp(T.ff[:, b], T.f33[:, b]), r=["f33_%d" % h], w=["ff%d" % h])
        for k in range(4 * h, 4 * h + 4):
            op("V", lambda k=k: V.transpose(T.tr[:, :, :, :, k], T.ff[:, 32 * k:32 * k + 32]), r=["ff%d" % h], w=["ts%d" % k] + (trs8 if k == 0 else []))
    for e in range(8):
        op("V", lambda e=e: V.transpose(T.Y[:, e:256:8], T.tr[:, :, e]), r=["ts%d" % k for k in range(8)], w=["Y%d" % e])
    dma("Y", T.ya[:], T.Y[:], "dya", r=["Y%d" % e for e in range(8)])
    for s, n in total.items():
        if seen["G"].get(s, 0) < n:
            g.wait_ge(T.sem[s], n)
